import numpy as np
import ml_dtypes


def mxq(x, axis, fmt="e4m3"):
    dtype, down = {"e4m3": (ml_dtypes.float8_e4m3fn, 7), "e5m2": (ml_dtypes.float8_e5m2, 14)}[fmt]
    v = np.moveaxis(np.asarray(x, np.float32).astype(ml_dtypes.bfloat16).astype(np.float64), axis, -1)
    blocks = v.reshape(v.shape[:-1] + (-1, 32))
    amax = np.abs(blocks).max(-1, keepdims=True)
    byte = np.maximum(np.where(amax > 0, np.frexp(amax)[1] - 1 + 127, 0) - down, 1)
    scale = np.exp2(byte - 127.0)
    codes = (blocks / scale).astype(np.float32).astype(dtype).astype(np.float64)
    return np.moveaxis((codes * scale).reshape(v.shape), -1, axis)


WIDE = False


def mx_kscale(k, group=512):
    if not WIDE:
        return np.ones(k)
    levels = np.array([10, -10, 5, -5, 0])
    if group != 512:
        return np.exp2(np.random.permutation(np.resize(levels, k // group))).repeat(group)
    if k % 512:
        return np.exp2(np.random.permutation(np.resize(levels, k // 32))).repeat(32)
    a = np.empty((k // 512, 16))
    for p in range(k // 512):
        a[p, :8] = np.random.permutation(np.resize(levels, 8))
        for g in range(8):
            far = levels[np.abs(levels - a[p, g]) >= 10]
            a[p, g + 8] = far[np.random.randint(len(far))]
    return np.exp2(a.ravel()).repeat(32)


def f64(x):
    return np.asarray(x).astype(np.float64)


G, D, K, M, N = 4, 256, 512, 128, 512


def setup_inputs():
    n = np.random.standard_normal
    s = mx_kscale(D, 0)[:, None]
    u = mx_kscale(K)[:, None]
    return {
        "x": (n((G, D, N)) * s).astype(np.float32),
        "w1": (n((G, D, K)) / np.sqrt(D) / s).astype(np.float32),
        "hs": (np.random.uniform(0.5, 2.0, (G, K, 1)) * u).astype(np.float32),
        "w2": (n((G, K, M)) / np.sqrt(K) / u).astype(np.float32),
        "b": (0.5 * n((G, K, 1))).astype(np.float32),
        "r": n((G, M, N)).astype(np.float32),
    }


def reference(x, w1, hs, w2, b, r):
    xq = mxq(f64(x), 1, "e4m3")
    h = mxq(f64(w1), 1, "e4m3").transpose(0, 2, 1) @ xq
    h = h + f64(b)
    h = (1.0 / (1.0 + np.exp(-(h)))) * f64(hs)
    y = mxq(f64(w2), 1, "e4m3").transpose(0, 2, 1) @ mxq(h, 1, "e4m3")
    y = y + f64(r)
    return y

@@ -1,0 +1,370 @@
+from contextlib import ExitStack
+
+import concourse.mybir as mybir
+
+G, D, K, M, N = 4, 256, 512, 128, 512
+FLOPS = 2 * G * N * K * (D + M)
+
+F32 = mybir.dt.float32
+BF16 = mybir.dt.bfloat16
+U32 = mybir.dt.uint32
+U8 = mybir.dt.uint8
+FP8X4 = mybir.dt.float8_e4m3fn_x4
+SIGMOID = mybir.ActivationFunctionType.Sigmoid
+COPY = mybir.ActivationFunctionType.Copy
+MULT = mybir.AluOpType.mult
+ADD = mybir.AluOpType.add
+
+P = 128
+PACK = 4
+ROWS = 64
+SETS = 2
+BANK = 512
+NMM = 128
+RUN = 4
+HRUN = 4
+Z_BANKS = 3
+
+W1_PARTS = [(0, 0, 256), (0, 256, 512), (1, 0, 512)]
+X_PARTS = [(0, 0, 256), (0, 256, 512), (1, 0, 256), (1, 256, 512)]
+PIECES = [(0, 0, 128), (0, 128, 256), (1, 0, 256), (0, 256, 512), (1, 256, 512), (2, 0, 256), (3, 0, 256), (2, 256, 512), (3, 256, 384), (3, 384, 512)]
+
+
+def tile_rows_gmlp_sigmoid_bias_res_kernel(tc, x, w1, hs, w2, b, r, out):
+    nc = tc.nc
+    with ExitStack() as ctx:
+        sb = ctx.enter_context(tc.tile_pool(name="sb", bufs=1))
+        ps = ctx.enter_context(tc.psum_pool(name="ps", bufs=1))
+        ctx.enter_context(tc.manual_schedule())
+
+        def tile(name, shape, dtype):
+            return sb.tile(shape, dtype, name=name, align_bytes=64)
+
+        w1_raw = [tile("w1_raw%d" % i, [P, PACK, hi - lo], F32) for i, (s, lo, hi) in enumerate(W1_PARTS)]
+        w1_bf = [tile("w1_bf%d" % i, [P, PACK * (hi - lo)], BF16) for i, (s, lo, hi) in enumerate(W1_PARTS)]
+        x_raw = [tile("x_raw%d" % i, [P, PACK, hi - lo], F32) for i, (s, lo, hi) in enumerate(X_PARTS)]
+        x_bf = [tile("x_bf%d" % i, [P, PACK * (hi - lo)], BF16) for i, (s, lo, hi) in enumerate(X_PARTS)]
+        x_codes = [tile("x_codes%d" % i, [P, hi - lo], U32) for i, (s, lo, hi) in enumerate(X_PARTS)]
+        x_scales = [tile("x_scales%d" % i, [P, hi - lo], U8) for i, (s, lo, hi) in enumerate(X_PARTS)]
+        w1_codes = [[tile("w1_codes%d%d" % (s, t), [P, P], U32) for t in range(PACK)] for s in range(SETS)]
+        w1_scales = [[tile("w1_scales%d%d" % (s, t), [P, P], U8) for t in range(PACK)] for s in range(SETS)]
+        w1_codes_whole = [tile("w1_codesw%d" % s, [P, K], U32) for s in range(SETS)]
+        w1_scales_whole = [tile("w1_scalesw%d" % s, [P, K], U8) for s in range(SETS)]
+        w2_raw = [tile("w2_raw%d" % s, [P, 2, PACK, M], F32) for s in range(SETS)]
+        w2_bf = [tile("w2_bf%d" % s, [P, 2 * PACK * M], BF16) for s in range(SETS)]
+        w2_codes = [tile("w2_codes%d" % s, [P, 2 * M], U32) for s in range(SETS)]
+        w2_scales = [tile("w2_scales%d" % s, [P, 2 * M], U8) for s in range(SETS)]
+        r_sb = [tile("r_sb%d" % g, [P, N], F32) for g in range(G)]
+        bias = tile("bias", [P, G, 8], F32)
+        gain = tile("gain", [P, G, 8], F32)
+        warm = tile("warm", [P, 16], F32)
+
+        sig = [tile("sig%d" % u, [P, PACK, hi - lo], F32) for u, (g, lo, hi) in enumerate(PIECES)]
+        h_pl = [tile("h_pl%d" % u, [P, PACK, hi - lo], BF16) for u, (g, lo, hi) in enumerate(PIECES)]
+        h_bf = [tile("h_bf%d" % u, [P, PACK * (hi - lo)], BF16) for u, (g, lo, hi) in enumerate(PIECES)]
+        h_codes = [tile("h_codes%d" % u, [P, hi - lo], U32) for u, (g, lo, hi) in enumerate(PIECES)]
+        h_scales = [tile("h_scales%d" % u, [P, hi - lo], U8) for u, (g, lo, hi) in enumerate(PIECES)]
+        y_sb = [tile("y_sb%d" % u, [P, hi - lo], F32) for u, (g, lo, hi) in enumerate(PIECES)]
+
+        z_banks = [[ps.tile([P, BANK], F32, name="z%d%d" % (c, i)) for i in range(Z_BANKS)] for c in range(2)]
+        y_banks = [ps.tile([P, BANK], F32, name="y%d" % i) for i in range(2)]
+
+        def pair(t, s):
+            return t[2 * s : 2 * s + 2].rearrange("g (p j) n -> (g p) j n", j=PACK)
+
+        def load_w1(i):
+            s, lo, hi = W1_PARTS[i]
+            nc.sync.dma_start(out=w1_raw[i][:], in_=pair(w1, s)[:, :, lo:hi])
+
+        def load_x(i):
+            s, lo, hi = X_PARTS[i]
+            nc.sync.dma_start(out=x_raw[i][:], in_=pair(x, s)[:, :, lo:hi])
+
+        def load_w2(s):
+            nc.sync.dma_start(
+                out=w2_raw[s][:].rearrange("p g j m -> p g (j m)"),
+                in_=w2[2 * s : 2 * s + 2].rearrange("g (p j) m -> p g (j m)", j=PACK),
+            )
+
+        def load_r(g):
+            nc.sync.dma_start(out=r_sb[g][:], in_=r[g])
+
+        def load_small(queue, dst, src):
+            queue.dma_start(out=dst[:, :, 0:PACK], in_=src.rearrange("g (p t) o -> p g (t o)", t=PACK))
+
+        def copy(engine, dst, src):
+            if engine == "V":
+                nc.vector.tensor_copy(out=dst, in_=src)
+            else:
+                nc.scalar.copy(out=dst, in_=src)
+
+        def round_w1(engine, i, a=0, z=None):
+            s, lo, hi = W1_PARTS[i]
+            z = (hi - lo) // PACK if z is None else z
+            copy(
+                engine,
+                w1_bf[i][:].rearrange("p (t m j) -> p m j t", t=PACK, j=PACK)[:, a:z],
+                w1_raw[i][:].rearrange("p j (m t) -> p m j t", t=PACK)[:, a:z],
+            )
+
+        def w1_operand(s, t):
+            if (s, 0, K) in W1_PARTS:
+                return w1_codes_whole[s][:, t * P : (t + 1) * P], w1_scales_whole[s][:, t * P : (t + 1) * P]
+            return w1_codes[s][t][:], w1_scales[s][t][:]
+
+        w1_done = []
+
+        def quant_w1(i):
+            s, lo, hi = W1_PARTS[i]
+            if hi - lo == K:
+                nc.vector.quantize_mx(out=w1_codes_whole[s][:].bitcast(FP8X4), scales=w1_scales_whole[s][:], in_=w1_bf[i][:])
+            else:
+                for t in range(PACK):
+                    cols = slice(lo // PACK, hi // PACK)
+                    nc.vector.quantize_mx(
+                        out=w1_codes[s][t][:, cols].bitcast(FP8X4),
+                        scales=w1_scales[s][t][:, cols],
+                        in_=w1_bf[i][:, t * (hi - lo) : (t + 1) * (hi - lo)],
+                    )
+            w1_done.append(i)
+            fill_banks()
+
+        def round_x(engine, i, a=0, z=None):
+            s, lo, hi = X_PARTS[i]
+            z = hi - lo if z is None else z
+            copy(
+                engine,
+                x_bf[i][:, PACK * a : PACK * z].rearrange("p (c i j) -> p c j i", i=RUN, j=PACK),
+                x_raw[i][:, :, a:z].rearrange("p j (c i) -> p c j i", i=RUN),
+            )
+
+        x_done = []
+
+        def quant_x(i):
+            nc.vector.quantize_mx(out=x_codes[i][:].bitcast(FP8X4), scales=x_scales[i][:], in_=x_bf[i][:])
+            x_done.append(i)
+            fill_banks()
+
+        def round_w2(engine, s, a=0, z=2):
+            copy(
+                engine,
+                w2_bf[s][:].rearrange("p (g c i j) -> p g c j i", g=2, i=RUN, j=PACK)[:, a:z],
+                w2_raw[s][:].rearrange("p g j (c i) -> p g c j i", i=RUN)[:, a:z],
+            )
+
+        def quant_w2(s):
+            nc.vector.quantize_mx(out=w2_codes[s][:].bitcast(FP8X4), scales=w2_scales[s][:], in_=w2_bf[s][:])
+
+        jobs = []
+        for u, (g, lo, hi) in enumerate(PIECES):
+            per_bank = BANK // (hi - lo)
+            jobs.extend((u, t0, per_bank) for t0 in range(0, PACK, per_bank))
+        bank_of = {}
+        count = [0, 0]
+        for job in jobs:
+            c = PIECES[job[0]][0] % 2
+            bank_of[job] = (c, count[c] % Z_BANKS)
+            count[c] = count[c] + 1
+        filled = []
+        emptied = []
+
+        def x_part(s, n0):
+            return [i for i, (ss, lo, hi) in enumerate(X_PARTS) if ss == s and lo <= n0 < hi][0]
+
+        def ready(job):
+            g, lo, hi = PIECES[job[0]]
+            s = g // 2
+            return (
+                all(i in w1_done for i, part in enumerate(W1_PARTS) if part[0] == s)
+                and all(x_part(s, n0) in x_done for n0 in range(lo, hi, NMM))
+                and all(other in emptied for other in filled if bank_of[other] == bank_of[job])
+            )
+
+        def fill_banks():
+            blocked = set()
+            for job in jobs:
+                c = bank_of[job][0]
+                if job in filled or c in blocked:
+                    continue
+                if not ready(job):
+                    blocked.add(c)
+                    continue
+                first_product(job)
+                filled.append(job)
+
+        def first_product(job):
+            u, t0, places = job
+            g, lo, hi = PIECES[u]
+            s, c = divmod(g, 2)
+            rows = slice(c * ROWS, (c + 1) * ROWS)
+            bank = z_banks[c][bank_of[job][1]]
+            for e in range(places):
+                codes, scales = w1_operand(s, t0 + e)
+                for n0 in range(lo, hi, NMM):
+                    i = x_part(s, n0)
+                    cols = slice(n0 - X_PARTS[i][1], n0 - X_PARTS[i][1] + NMM)
+                    at = e * (hi - lo) + n0 - lo
+                    nc.tensor.matmul_mx(
+                        out=bank[:, at : at + NMM],
+                        lhsT=codes[rows, :].bitcast(FP8X4),
+                        lhsT_scale=scales[rows, :],
+                        rhs=x_codes[i][rows, cols].bitcast(FP8X4),
+                        rhs_scale=x_scales[i][rows, cols],
+                        start=True,
+                        stop=True,
+                    )
+
+        def sigmoid(u):
+            g, lo, hi = PIECES[u]
+            for job in jobs:
+                if job[0] != u:
+                    continue
+                assert job in filled
+                c, i = bank_of[job]
+                for e in range(job[2]):
+                    t = job[1] + e
+                    nc.scalar.activation(
+                        out=sig[u][:, t, :],
+                        in_=z_banks[c][i][:, e * (hi - lo) : (e + 1) * (hi - lo)],
+                        func=SIGMOID,
+                        bias=bias[:, g, t : t + 1],
+                    )
+                emptied.append(job)
+                fill_banks()
+
+        def scale_h(u):
+            g, lo, hi = PIECES[u]
+            nc.vector.tensor_tensor(
+                out=h_bf[u][:].rearrange("p (c i t) -> p c t i", i=HRUN, t=PACK),
+                in0=sig[u][:].rearrange("p t (c i) -> p c t i", i=HRUN),
+                in1=gain[:, g, 0:PACK].unsqueeze(1).unsqueeze(3).to_broadcast([P, (hi - lo) // HRUN, PACK, HRUN]),
+                op=MULT,
+            )
+
+        def scale_h_on_scalar(u):
+            g, lo, hi = PIECES[u]
+            for t in range(PACK):
+                nc.scalar.activation(out=h_pl[u][:, t, :], in_=sig[u][:, t, :], func=COPY, scale=gain[:, g, t : t + 1])
+
+        def weave_h(engine, u):
+            copy(
+                engine,
+                h_bf[u][:].rearrange("p (c i t) -> p c t i", i=RUN, t=PACK),
+                h_pl[u][:].rearrange("p t (c i) -> p c t i", i=RUN),
+            )
+
+        def quant_h(u):
+            nc.vector.quantize_mx(out=h_codes[u][:].bitcast(FP8X4), scales=h_scales[u][:], in_=h_bf[u][:])
+
+        y_bank_of = {}
+
+        def second_product(u):
+            g, lo, hi = PIECES[u]
+            s, c = divmod(g, 2)
+            y_bank_of[u] = y_banks[len(y_bank_of) % 2]
+            for n0 in range(0, hi - lo, NMM):
+                nc.tensor.matmul_mx(
+                    out=y_bank_of[u][:, n0 : n0 + NMM],
+                    lhsT=w2_codes[s][:, c * M : (c + 1) * M].bitcast(FP8X4),
+                    lhsT_scale=w2_scales[s][:, c * M : (c + 1) * M],
+                    rhs=h_codes[u][:, n0 : n0 + NMM].bitcast(FP8X4),
+                    rhs_scale=h_scales[u][:, n0 : n0 + NMM],
+                    start=True,
+                    stop=True,
+                )
+
+        def finish(u):
+            g, lo, hi = PIECES[u]
+            nc.vector.tensor_tensor(out=y_sb[u][:], in0=y_bank_of[u][:, 0 : hi - lo], in1=r_sb[g][:, lo:hi], op=ADD)
+            nc.sync.dma_start(out=out[g][:, lo:hi], in_=y_sb[u][:])
+
+        def warm_up():
+            nc.vector.memset(warm[:, 0:8], 0.0)
+            nc.scalar.activation(out=warm[:, 8:9], in_=warm[:, 0:1], func=SIGMOID)
+
+        warm_up()
+        load_x(0)
+        load_w1(0)
+        load_w1(1)
+        load_small(nc.sync, bias, b)
+        load_x(1)
+        load_small(nc.sync, gain, hs)
+        load_w1(2)
+        load_x(2)
+        load_w2(0)
+        load_x(3)
+        load_r(0)
+        load_r(1)
+        load_w2(1)
+        load_r(2)
+        load_r(3)
+        round_x("V", 0)
+        quant_x(0)
+        round_w1("V", 0)
+        quant_w1(0)
+        round_w1("V", 1, 0, 44)
+        round_w1("S", 1, 44, 64)
+        quant_w1(1)
+        round_x("V", 1)
+        sigmoid(0)
+        sigmoid(1)
+        quant_x(1)
+        scale_h(0)
+        scale_h(1)
+        quant_h(0)
+        sigmoid(2)
+        round_w1("V", 2, 0, 64)
+        round_w1("S", 2, 64, 128)
+        quant_h(1)
+        scale_h(2)
+        quant_w1(2)
+        sigmoid(3)
+        quant_h(2)
+        round_x("S", 2)
+        scale_h(3)
+        quant_x(2)
+        sigmoid(4)
+        quant_h(3)
+        round_w2("S", 0)
+        scale_h(4)
+        quant_w2(0)
+        second_product(0)
+        second_product(1)
+        sigmoid(5)
+        quant_h(4)
+        finish(0)
+        finish(1)
+        second_product(2)
+        second_product(3)
+        round_x("S", 3)
+        scale_h(5)
+        quant_x(3)
+        sigmoid(6)
+        quant_h(5)
+        finish(2)
+        finish(3)
+        second_product(4)
+        round_w2("S", 1)
+        scale_h(6)
+        quant_w2(1)
+        second_product(5)
+        sigmoid(7)
+        quant_h(6)
+        finish(4)
+        finish(5)
+        second_product(6)
+        scale_h(7)
+        sigmoid(8)
+        sigmoid(9)
+        finish(6)
+        quant_h(7)
+        second_product(7)
+        scale_h(8)
+        scale_h(9)
+        quant_h(8)
+        second_product(8)
+        finish(7)
+        quant_h(9)
+        second_product(9)
+        finish(8)
+        finish(9)

@@ -21,13 +21,15 @@ ROWS = 64
 SETS = 2
 BANK = 512
 NMM = 128
-RUN = 4
-HRUN = 4
+RUN = 2
+HRUN = 2
 Z_BANKS = 3
 
 W1_PARTS = [(0, 0, 256), (0, 256, 512), (1, 0, 512)]
 X_PARTS = [(0, 0, 256), (0, 256, 512), (1, 0, 256), (1, 256, 512)]
 PIECES = [(0, 0, 128), (0, 128, 256), (1, 0, 256), (0, 256, 512), (1, 256, 512), (2, 0, 256), (3, 0, 256), (2, 256, 512), (3, 256, 384), (3, 384, 512)]
+OUTS = [(0, 0, 512), (1, 0, 512), (2, 0, 512), (3, 0, 384), (3, 384, 512)]
+X_LOADS = [(0, 0, 256), (0, 256, 512), (1, 0, 512)]
 
 
 def tile_rows_gmlp_sigmoid_bias_res_kernel(tc, x, w1, hs, w2, b, r, out):
@@ -42,7 +44,7 @@ def tile_rows_gmlp_sigmoid_bias_res_kernel(tc, x, w1, hs, w2, b, r, out):
 
         w1_raw = [tile("w1_raw%d" % i, [P, PACK, hi - lo], F32) for i, (s, lo, hi) in enumerate(W1_PARTS)]
         w1_bf = [tile("w1_bf%d" % i, [P, PACK * (hi - lo)], BF16) for i, (s, lo, hi) in enumerate(W1_PARTS)]
-        x_raw = [tile("x_raw%d" % i, [P, PACK, hi - lo], F32) for i, (s, lo, hi) in enumerate(X_PARTS)]
+        x_raw = [tile("x_raw%d" % i, [P, PACK, hi - lo], F32) for i, (s, lo, hi) in enumerate(X_LOADS)]
         x_bf = [tile("x_bf%d" % i, [P, PACK * (hi - lo)], BF16) for i, (s, lo, hi) in enumerate(X_PARTS)]
         x_codes = [tile("x_codes%d" % i, [P, hi - lo], U32) for i, (s, lo, hi) in enumerate(X_PARTS)]
         x_scales = [tile("x_scales%d" % i, [P, hi - lo], U8) for i, (s, lo, hi) in enumerate(X_PARTS)]
@@ -58,13 +60,16 @@ def tile_rows_gmlp_sigmoid_bias_res_kernel(tc, x, w1, hs, w2, b, r, out):
         bias = tile("bias", [P, G, 8], F32)
         gain = tile("gain", [P, G, 8], F32)
         warm = tile("warm", [P, 16], F32)
+        vec_rows = tile("vec_rows", [P, 2 * P], F32)
+        vec_dealt = tile("vec_dealt", [P, 2 * P], F32)
+        vec_turned = tile("vec_turned", [P, 2 * P], F32)
 
         sig = [tile("sig%d" % u, [P, PACK, hi - lo], F32) for u, (g, lo, hi) in enumerate(PIECES)]
         h_pl = [tile("h_pl%d" % u, [P, PACK, hi - lo], BF16) for u, (g, lo, hi) in enumerate(PIECES)]
         h_bf = [tile("h_bf%d" % u, [P, PACK * (hi - lo)], BF16) for u, (g, lo, hi) in enumerate(PIECES)]
         h_codes = [tile("h_codes%d" % u, [P, hi - lo], U32) for u, (g, lo, hi) in enumerate(PIECES)]
         h_scales = [tile("h_scales%d" % u, [P, hi - lo], U8) for u, (g, lo, hi) in enumerate(PIECES)]
-        y_sb = [tile("y_sb%d" % u, [P, hi - lo], F32) for u, (g, lo, hi) in enumerate(PIECES)]
+        y_sb = [tile("y_sb%d" % u, [P, hi - lo], F32) for u, (g, lo, hi) in enumerate(OUTS)]
 
         z_banks = [[ps.tile([P, BANK], F32, name="z%d%d" % (c, i)) for i in range(Z_BANKS)] for c in range(2)]
         y_banks = [ps.tile([P, BANK], F32, name="y%d" % i) for i in range(2)]
@@ -77,7 +82,7 @@ def tile_rows_gmlp_sigmoid_bias_res_kernel(tc, x, w1, hs, w2, b, r, out):
             nc.sync.dma_start(out=w1_raw[i][:], in_=pair(w1, s)[:, :, lo:hi])
 
         def load_x(i):
-            s, lo, hi = X_PARTS[i]
+            s, lo, hi = X_LOADS[i]
             nc.sync.dma_start(out=x_raw[i][:], in_=pair(x, s)[:, :, lo:hi])
 
         def load_w2(s):
@@ -103,8 +108,8 @@ def tile_rows_gmlp_sigmoid_bias_res_kernel(tc, x, w1, hs, w2, b, r, out):
             z = (hi - lo) // PACK if z is None else z
             copy(
                 engine,
-                w1_bf[i][:].rearrange("p (t m j) -> p m j t", t=PACK, j=PACK)[:, a:z],
-                w1_raw[i][:].rearrange("p j (m t) -> p m j t", t=PACK)[:, a:z],
+                w1_bf[i][:].rearrange("p (u e m j) -> p u m j e", u=2, e=2, j=PACK)[:, :, a:z],
+                w1_raw[i][:].rearrange("p j (m u e) -> p u m j e", u=2, e=2)[:, :, a:z],
             )
 
         def w1_operand(s, t):
@@ -132,10 +137,12 @@ def tile_rows_gmlp_sigmoid_bias_res_kernel(tc, x, w1, hs, w2, b, r, out):
         def round_x(engine, i, a=0, z=None):
             s, lo, hi = X_PARTS[i]
             z = hi - lo if z is None else z
+            load = [k for k, (ss, l0, l1) in enumerate(X_LOADS) if ss == s and l0 <= lo < l1][0]
+            off = lo - X_LOADS[load][1]
             copy(
                 engine,
                 x_bf[i][:, PACK * a : PACK * z].rearrange("p (c i j) -> p c j i", i=RUN, j=PACK),
-                x_raw[i][:, :, a:z].rearrange("p j (c i) -> p c j i", i=RUN),
+                x_raw[load][:, :, off + a : off + z].rearrange("p j (c i) -> p c j i", i=RUN),
             )
 
         x_done = []
@@ -256,15 +263,14 @@ def tile_rows_gmlp_sigmoid_bias_res_kernel(tc, x, w1, hs, w2, b, r, out):
         def quant_h(u):
             nc.vector.quantize_mx(out=h_codes[u][:].bitcast(FP8X4), scales=h_scales[u][:], in_=h_bf[u][:])
 
-        y_bank_of = {}
-
         def second_product(u):
             g, lo, hi = PIECES[u]
             s, c = divmod(g, 2)
-            y_bank_of[u] = y_banks[len(y_bank_of) % 2]
+            o = [k for k, (gg, l0, l1) in enumerate(OUTS) if gg == g and l0 <= lo < l1][0]
+            at = lo - OUTS[o][1]
             for n0 in range(0, hi - lo, NMM):
                 nc.tensor.matmul_mx(
-                    out=y_bank_of[u][:, n0 : n0 + NMM],
+                    out=y_banks[o % 2][:, at + n0 : at + n0 + NMM],
                     lhsT=w2_codes[s][:, c * M : (c + 1) * M].bitcast(FP8X4),
                     lhsT_scale=w2_scales[s][:, c * M : (c + 1) * M],
                     rhs=h_codes[u][:, n0 : n0 + NMM].bitcast(FP8X4),
@@ -273,34 +279,53 @@ def tile_rows_gmlp_sigmoid_bias_res_kernel(tc, x, w1, hs, w2, b, r, out):
                     stop=True,
                 )
 
-        def finish(u):
-            g, lo, hi = PIECES[u]
-            nc.vector.tensor_tensor(out=y_sb[u][:], in0=y_bank_of[u][:, 0 : hi - lo], in1=r_sb[g][:, lo:hi], op=ADD)
-            nc.sync.dma_start(out=out[g][:, lo:hi], in_=y_sb[u][:])
+        def finish(o, queue=nc.sync):
+            g, lo, hi = OUTS[o]
+            nc.vector.tensor_tensor(out=y_sb[o][:], in0=y_banks[o % 2][:, 0 : hi - lo], in1=r_sb[g][:, lo:hi], op=ADD)
+            queue.dma_start(out=out[g][:, lo:hi], in_=y_sb[o][:])
+
+        def load_vectors():
+            nc.vector.memset(vec_rows[:], 0.0)
+            for v, src in enumerate((b, hs)):
+                nc.scalar.dma_start(
+                    out=vec_rows[0:P:8, v * P : (v + 1) * P], in_=src.rearrange("g (q a) o -> q g (a o)", q=4)
+                )
+
+        def turn_vectors():
+            nc.vector.tensor_copy(
+                out=vec_dealt[:].rearrange("p (v t s) -> p v t s", v=2, t=PACK),
+                in_=vec_rows[:].rearrange("p (v s t) -> p v t s", v=2, t=PACK),
+            )
+            nc.vector.transpose(out=vec_turned[:], in_=vec_dealt[:])
+            for v, dst in enumerate((bias, gain)):
+                nc.vector.tensor_copy(
+                    out=dst[:, :, 0:PACK],
+                    in_=vec_turned[:, v * P : (v + 1) * P].rearrange("p (t g z) -> p g t z", t=PACK, g=G)[:, :, :, 0],
+                )
 
         def warm_up():
             nc.vector.memset(warm[:, 0:8], 0.0)
             nc.scalar.activation(out=warm[:, 8:9], in_=warm[:, 0:1], func=SIGMOID)
 
-        warm_up()
+        load_vectors()
         load_x(0)
+        warm_up()
         load_w1(0)
         load_w1(1)
-        load_small(nc.sync, bias, b)
         load_x(1)
-        load_small(nc.sync, gain, hs)
         load_w1(2)
         load_x(2)
         load_w2(0)
-        load_x(3)
         load_r(0)
-        load_r(1)
         load_w2(1)
+        load_r(1)
         load_r(2)
         load_r(3)
+        turn_vectors()
         round_x("V", 0)
         quant_x(0)
-        round_w1("V", 0)
+        round_w1("V", 0, 0, 44)
+        round_w1("S", 0, 44, 64)
         quant_w1(0)
         round_w1("V", 1, 0, 44)
         round_w1("S", 1, 44, 64)
@@ -325,46 +350,42 @@ def tile_rows_gmlp_sigmoid_bias_res_kernel(tc, x, w1, hs, w2, b, r, out):
         quant_x(2)
         sigmoid(4)
         quant_h(3)
-        round_w2("S", 0)
+        round_w2("V", 0, 0, 1)
+        round_w2("S", 0, 1, 2)
         scale_h(4)
         quant_w2(0)
+        sigmoid(5)
         second_product(0)
         second_product(1)
-        sigmoid(5)
-        quant_h(4)
-        finish(0)
-        finish(1)
-        second_product(2)
         second_product(3)
+        quant_h(4)
         round_x("S", 3)
+        second_product(2)
+        second_product(4)
         scale_h(5)
         quant_x(3)
+        finish(0)
         sigmoid(6)
         quant_h(5)
-        finish(2)
-        finish(3)
-        second_product(4)
+        finish(1)
         round_w2("S", 1)
         scale_h(6)
         quant_w2(1)
-        second_product(5)
         sigmoid(7)
+        second_product(5)
         quant_h(6)
-        finish(4)
-        finish(5)
         second_product(6)
         scale_h(7)
         sigmoid(8)
         sigmoid(9)
-        finish(6)
         quant_h(7)
         second_product(7)
         scale_h(8)
-        scale_h(9)
+        finish(2)
         quant_h(8)
         second_product(8)
-        finish(7)
+        scale_h(9)
+        finish(3)
         quant_h(9)
         second_product(9)
-        finish(8)
-        finish(9)
+        finish(4)

@@ -25,10 +25,10 @@ RUN = 2
 HRUN = 2
 Z_BANKS = 3
 
-W1_PARTS = [(0, 0, 256), (0, 256, 512), (1, 0, 512)]
-X_PARTS = [(0, 0, 256), (0, 256, 512), (1, 0, 256), (1, 256, 512)]
+W1_PARTS = [(0, 0, 512), (1, 0, 512)]
+X_PARTS = [(0, 0, 128), (0, 128, 256), (0, 256, 512), (1, 0, 256), (1, 256, 512)]
 PIECES = [(0, 0, 128), (0, 128, 256), (1, 0, 256), (0, 256, 512), (1, 256, 512), (2, 0, 256), (3, 0, 256), (2, 256, 512), (3, 256, 384), (3, 384, 512)]
-OUTS = [(0, 0, 512), (1, 0, 512), (2, 0, 512), (3, 0, 384), (3, 384, 512)]
+OUTS = [(0, 0, 512), (1, 0, 512), (2, 0, 256), (3, 0, 256), (2, 256, 512), (3, 256, 512)]
 X_LOADS = [(0, 0, 256), (0, 256, 512), (1, 0, 512)]
 
 
@@ -234,7 +234,7 @@ def tile_rows_gmlp_sigmoid_bias_res_kernel(tc, x, w1, hs, w2, b, r, out):
                         out=sig[u][:, t, :],
                         in_=z_banks[c][i][:, e * (hi - lo) : (e + 1) * (hi - lo)],
                         func=SIGMOID,
-                        bias=bias[:, g, t : t + 1],
+                        bias=vec_turned[:, 32 * t + 8 * g : 32 * t + 8 * g + 1],
                     )
                 emptied.append(job)
                 fill_banks()
@@ -285,35 +285,37 @@ def tile_rows_gmlp_sigmoid_bias_res_kernel(tc, x, w1, hs, w2, b, r, out):
             queue.dma_start(out=out[g][:, lo:hi], in_=y_sb[o][:])
 
         def load_vectors():
-            nc.vector.memset(vec_rows[:], 0.0)
             for v, src in enumerate((b, hs)):
-                nc.scalar.dma_start(
+                nc.sync.dma_start(
                     out=vec_rows[0:P:8, v * P : (v + 1) * P], in_=src.rearrange("g (q a) o -> q g (a o)", q=4)
                 )
 
-        def turn_vectors():
+        def deal_vectors():
             nc.vector.tensor_copy(
                 out=vec_dealt[:].rearrange("p (v t s) -> p v t s", v=2, t=PACK),
                 in_=vec_rows[:].rearrange("p (v s t) -> p v t s", v=2, t=PACK),
             )
+
+        def turn_vectors():
             nc.vector.transpose(out=vec_turned[:], in_=vec_dealt[:])
-            for v, dst in enumerate((bias, gain)):
-                nc.vector.tensor_copy(
-                    out=dst[:, :, 0:PACK],
-                    in_=vec_turned[:, v * P : (v + 1) * P].rearrange("p (t g z) -> p g t z", t=PACK, g=G)[:, :, :, 0],
-                )
+
+        def gather_gain():
+            nc.vector.tensor_copy(
+                out=gain[:, :, 0:PACK],
+                in_=vec_turned[:, P : 2 * P].rearrange("p (t g z) -> p g t z", t=PACK, g=G)[:, :, :, 0],
+            )
 
         def warm_up():
             nc.vector.memset(warm[:, 0:8], 0.0)
+            nc.vector.memset(vec_rows[:], 0.0)
             nc.scalar.activation(out=warm[:, 8:9], in_=warm[:, 0:1], func=SIGMOID)
 
-        load_vectors()
-        load_x(0)
         warm_up()
         load_w1(0)
-        load_w1(1)
+        load_vectors()
+        load_x(0)
         load_x(1)
-        load_w1(2)
+        load_w1(1)
         load_x(2)
         load_w2(0)
         load_r(0)
@@ -321,37 +323,37 @@ def tile_rows_gmlp_sigmoid_bias_res_kernel(tc, x, w1, hs, w2, b, r, out):
         load_r(1)
         load_r(2)
         load_r(3)
-        turn_vectors()
-        round_x("V", 0)
-        quant_x(0)
-        round_w1("V", 0, 0, 44)
-        round_w1("S", 0, 44, 64)
+        round_w1("V", 0, 0, 80)
+        round_w1("S", 0, 80, 128)
+        deal_vectors()
         quant_w1(0)
-        round_w1("V", 1, 0, 44)
-        round_w1("S", 1, 44, 64)
-        quant_w1(1)
-        round_x("V", 1)
+        round_x("V", 0)
+        round_x("S", 1)
+        turn_vectors()
+        quant_x(0)
+        quant_x(1)
+        gather_gain()
+        round_x("V", 2)
         sigmoid(0)
         sigmoid(1)
-        quant_x(1)
         scale_h(0)
+        quant_x(2)
         scale_h(1)
         quant_h(0)
         sigmoid(2)
-        round_w1("V", 2, 0, 64)
-        round_w1("S", 2, 64, 128)
+        round_w1("V", 1, 0, 64)
+        round_w1("S", 1, 64, 128)
         quant_h(1)
         scale_h(2)
-        quant_w1(2)
+        quant_w1(1)
         sigmoid(3)
         quant_h(2)
-        round_x("S", 2)
+        round_x("S", 3)
         scale_h(3)
-        quant_x(2)
+        quant_x(3)
         sigmoid(4)
         quant_h(3)
-        round_w2("V", 0, 0, 1)
-        round_w2("S", 0, 1, 2)
+        round_w2("V", 0)
         scale_h(4)
         quant_w2(0)
         sigmoid(5)
@@ -359,33 +361,35 @@ def tile_rows_gmlp_sigmoid_bias_res_kernel(tc, x, w1, hs, w2, b, r, out):
         second_product(1)
         second_product(3)
         quant_h(4)
-        round_x("S", 3)
+        round_x("S", 4)
         second_product(2)
         second_product(4)
         scale_h(5)
-        quant_x(3)
-        finish(0)
+        quant_x(4)
         sigmoid(6)
+        finish(0)
         quant_h(5)
-        finish(1)
         round_w2("S", 1)
         scale_h(6)
         quant_w2(1)
         sigmoid(7)
         second_product(5)
+        finish(1)
         quant_h(6)
         second_product(6)
+        finish(2)
         scale_h(7)
         sigmoid(8)
         sigmoid(9)
+        scale_h_on_scalar(9)
+        weave_h("S", 9)
+        finish(3)
         quant_h(7)
         second_product(7)
         scale_h(8)
-        finish(2)
+        finish(4)
         quant_h(8)
         second_product(8)
-        scale_h(9)
-        finish(3)
         quant_h(9)
         second_product(9)
-        finish(4)
+        finish(5)

@@ -18,18 +18,12 @@ ADD = mybir.AluOpType.add
 P = 128
 PACK = 4
 ROWS = 64
-SETS = 2
-BANK = 512
-NMM = 128
+PAIRS = 2
+HALF = N // 2
 RUN = 2
 HRUN = 2
 Z_BANKS = 3
-
-W1_PARTS = [(0, 0, 512), (1, 0, 512)]
-X_PARTS = [(0, 0, 128), (0, 128, 256), (0, 256, 512), (1, 0, 256), (1, 256, 512)]
-PIECES = [(0, 0, 128), (0, 128, 256), (1, 0, 256), (0, 256, 512), (1, 256, 512), (2, 0, 256), (3, 0, 256), (2, 256, 512), (3, 256, 384), (3, 384, 512)]
-OUTS = [(0, 0, 512), (1, 0, 512), (2, 0, 256), (3, 0, 256), (2, 256, 512), (3, 256, 512)]
-X_LOADS = [(0, 0, 256), (0, 256, 512), (1, 0, 512)]
+WIDTH = [256, 256, 256, 128]
 
 
 def tile_rows_gmlp_sigmoid_bias_res_kernel(tc, x, w1, hs, w2, b, r, out):
@@ -42,48 +36,42 @@ def tile_rows_gmlp_sigmoid_bias_res_kernel(tc, x, w1, hs, w2, b, r, out):
         def tile(name, shape, dtype):
             return sb.tile(shape, dtype, name=name, align_bytes=64)
 
-        w1_raw = [tile("w1_raw%d" % i, [P, PACK, hi - lo], F32) for i, (s, lo, hi) in enumerate(W1_PARTS)]
-        w1_bf = [tile("w1_bf%d" % i, [P, PACK * (hi - lo)], BF16) for i, (s, lo, hi) in enumerate(W1_PARTS)]
-        x_raw = [tile("x_raw%d" % i, [P, PACK, hi - lo], F32) for i, (s, lo, hi) in enumerate(X_LOADS)]
-        x_bf = [tile("x_bf%d" % i, [P, PACK * (hi - lo)], BF16) for i, (s, lo, hi) in enumerate(X_PARTS)]
-        x_codes = [tile("x_codes%d" % i, [P, hi - lo], U32) for i, (s, lo, hi) in enumerate(X_PARTS)]
-        x_scales = [tile("x_scales%d" % i, [P, hi - lo], U8) for i, (s, lo, hi) in enumerate(X_PARTS)]
-        w1_codes = [[tile("w1_codes%d%d" % (s, t), [P, P], U32) for t in range(PACK)] for s in range(SETS)]
-        w1_scales = [[tile("w1_scales%d%d" % (s, t), [P, P], U8) for t in range(PACK)] for s in range(SETS)]
-        w1_codes_whole = [tile("w1_codesw%d" % s, [P, K], U32) for s in range(SETS)]
-        w1_scales_whole = [tile("w1_scalesw%d" % s, [P, K], U8) for s in range(SETS)]
-        w2_raw = [tile("w2_raw%d" % s, [P, 2, PACK, M], F32) for s in range(SETS)]
-        w2_bf = [tile("w2_bf%d" % s, [P, 2 * PACK * M], BF16) for s in range(SETS)]
-        w2_codes = [tile("w2_codes%d" % s, [P, 2 * M], U32) for s in range(SETS)]
-        w2_scales = [tile("w2_scales%d" % s, [P, 2 * M], U8) for s in range(SETS)]
+        w1_raw = [tile("w1_raw%d" % s, [P, PACK, K], F32) for s in range(PAIRS)]
+        w1_bf = [[tile("w1_bf%d%d" % (s, u), [P, 2 * PACK * P], BF16) for u in range(2)] for s in range(PAIRS)]
+        w1_codes = [[tile("w1_codes%d%d" % (s, t), [P, P], U32) for t in range(PACK)] for s in range(PAIRS)]
+        w1_scales = [[tile("w1_scales%d%d" % (s, t), [P, P], U8) for t in range(PACK)] for s in range(PAIRS)]
+        x_raw = [tile("x_raw%d" % s, [P, PACK, N], F32) for s in range(PAIRS)]
+        x_bf = [tile("x_bf%d" % s, [P, PACK * N], BF16) for s in range(PAIRS)]
+        x_codes = [tile("x_codes%d" % s, [P, N], U32) for s in range(PAIRS)]
+        x_scales = [tile("x_scales%d" % s, [P, N], U8) for s in range(PAIRS)]
+        w2_raw = [tile("w2_raw%d" % s, [P, 2, PACK, M], F32) for s in range(PAIRS)]
+        w2_bf = [tile("w2_bf%d" % g, [P, PACK * M], BF16) for g in range(G)]
+        w2_codes = [tile("w2_codes%d" % g, [P, M], U32) for g in range(G)]
+        w2_scales = [tile("w2_scales%d" % g, [P, M], U8) for g in range(G)]
         r_sb = [tile("r_sb%d" % g, [P, N], F32) for g in range(G)]
-        bias = tile("bias", [P, G, 8], F32)
-        gain = tile("gain", [P, G, 8], F32)
-        warm = tile("warm", [P, 16], F32)
         vec_rows = tile("vec_rows", [P, 2 * P], F32)
         vec_dealt = tile("vec_dealt", [P, 2 * P], F32)
         vec_turned = tile("vec_turned", [P, 2 * P], F32)
+        gain = tile("gain", [P, G, PACK], F32)
 
-        sig = [tile("sig%d" % u, [P, PACK, hi - lo], F32) for u, (g, lo, hi) in enumerate(PIECES)]
-        h_pl = [tile("h_pl%d" % u, [P, PACK, hi - lo], BF16) for u, (g, lo, hi) in enumerate(PIECES)]
-        h_bf = [tile("h_bf%d" % u, [P, PACK * (hi - lo)], BF16) for u, (g, lo, hi) in enumerate(PIECES)]
-        h_codes = [tile("h_codes%d" % u, [P, hi - lo], U32) for u, (g, lo, hi) in enumerate(PIECES)]
-        h_scales = [tile("h_scales%d" % u, [P, hi - lo], U8) for u, (g, lo, hi) in enumerate(PIECES)]
-        y_sb = [tile("y_sb%d" % u, [P, hi - lo], F32) for u, (g, lo, hi) in enumerate(OUTS)]
+        sig = [tile("sig%d" % g, [P, N // WIDTH[g], PACK, WIDTH[g]], F32) for g in range(G)]
+        h_rows = {(g, a): tile("h_rows%d%d" % (g, a), [P, PACK, WIDTH[g]], BF16) for g in range(G) for a in range(N // WIDTH[g])}
+        h_bf = [[tile("h_bf%d%d" % (g, a), [P, PACK * WIDTH[g]], BF16) for a in range(N // WIDTH[g])] for g in range(G)]
+        h_codes = [tile("h_codes%d" % g, [P, N], U32) for g in range(G)]
+        h_scales = [tile("h_scales%d" % g, [P, N], U8) for g in range(G)]
+        y_sb = {(g, lo): tile("y_sb%d_%d" % (g, lo), [P, N], F32) for g in range(G) for lo in (0, 128, 256, 384)}
 
-        z_banks = [[ps.tile([P, BANK], F32, name="z%d%d" % (c, i)) for i in range(Z_BANKS)] for c in range(2)]
-        y_banks = [ps.tile([P, BANK], F32, name="y%d" % i) for i in range(2)]
+        z_banks = [[ps.tile([P, N], F32, name="z%d%d" % (c, i)) for i in range(Z_BANKS)] for c in range(2)]
+        y_banks = [ps.tile([P, N], F32, name="y%d" % i) for i in range(2)]
 
         def pair(t, s):
             return t[2 * s : 2 * s + 2].rearrange("g (p j) n -> (g p) j n", j=PACK)
 
-        def load_w1(i):
-            s, lo, hi = W1_PARTS[i]
-            nc.sync.dma_start(out=w1_raw[i][:], in_=pair(w1, s)[:, :, lo:hi])
+        def load_w1(s):
+            nc.sync.dma_start(out=w1_raw[s][:], in_=pair(w1, s))
 
-        def load_x(i):
-            s, lo, hi = X_LOADS[i]
-            nc.sync.dma_start(out=x_raw[i][:], in_=pair(x, s)[:, :, lo:hi])
+        def load_x(s):
+            nc.sync.dma_start(out=x_raw[s][:], in_=pair(x, s))
 
         def load_w2(s):
             nc.sync.dma_start(
@@ -93,196 +81,6 @@ def tile_rows_gmlp_sigmoid_bias_res_kernel(tc, x, w1, hs, w2, b, r, out):
 
         def load_r(g):
             nc.sync.dma_start(out=r_sb[g][:], in_=r[g])
-
-        def load_small(queue, dst, src):
-            queue.dma_start(out=dst[:, :, 0:PACK], in_=src.rearrange("g (p t) o -> p g (t o)", t=PACK))
-
-        def copy(engine, dst, src):
-            if engine == "V":
-                nc.vector.tensor_copy(out=dst, in_=src)
-            else:
-                nc.scalar.copy(out=dst, in_=src)
-
-        def round_w1(engine, i, a=0, z=None):
-            s, lo, hi = W1_PARTS[i]
-            z = (hi - lo) // PACK if z is None else z
-            copy(
-                engine,
-                w1_bf[i][:].rearrange("p (u e m j) -> p u m j e", u=2, e=2, j=PACK)[:, :, a:z],
-                w1_raw[i][:].rearrange("p j (m u e) -> p u m j e", u=2, e=2)[:, :, a:z],
-            )
-
-        def w1_operand(s, t):
-            if (s, 0, K) in W1_PARTS:
-                return w1_codes_whole[s][:, t * P : (t + 1) * P], w1_scales_whole[s][:, t * P : (t + 1) * P]
-            return w1_codes[s][t][:], w1_scales[s][t][:]
-
-        w1_done = []
-
-        def quant_w1(i):
-            s, lo, hi = W1_PARTS[i]
-            if hi - lo == K:
-                nc.vector.quantize_mx(out=w1_codes_whole[s][:].bitcast(FP8X4), scales=w1_scales_whole[s][:], in_=w1_bf[i][:])
-            else:
-                for t in range(PACK):
-                    cols = slice(lo // PACK, hi // PACK)
-                    nc.vector.quantize_mx(
-                        out=w1_codes[s][t][:, cols].bitcast(FP8X4),
-                        scales=w1_scales[s][t][:, cols],
-                        in_=w1_bf[i][:, t * (hi - lo) : (t + 1) * (hi - lo)],
-                    )
-            w1_done.append(i)
-            fill_banks()
-
-        def round_x(engine, i, a=0, z=None):
-            s, lo, hi = X_PARTS[i]
-            z = hi - lo if z is None else z
-            load = [k for k, (ss, l0, l1) in enumerate(X_LOADS) if ss == s and l0 <= lo < l1][0]
-            off = lo - X_LOADS[load][1]
-            copy(
-                engine,
-                x_bf[i][:, PACK * a : PACK * z].rearrange("p (c i j) -> p c j i", i=RUN, j=PACK),
-                x_raw[load][:, :, off + a : off + z].rearrange("p j (c i) -> p c j i", i=RUN),
-            )
-
-        x_done = []
-
-        def quant_x(i):
-            nc.vector.quantize_mx(out=x_codes[i][:].bitcast(FP8X4), scales=x_scales[i][:], in_=x_bf[i][:])
-            x_done.append(i)
-            fill_banks()
-
-        def round_w2(engine, s, a=0, z=2):
-            copy(
-                engine,
-                w2_bf[s][:].rearrange("p (g c i j) -> p g c j i", g=2, i=RUN, j=PACK)[:, a:z],
-                w2_raw[s][:].rearrange("p g j (c i) -> p g c j i", i=RUN)[:, a:z],
-            )
-
-        def quant_w2(s):
-            nc.vector.quantize_mx(out=w2_codes[s][:].bitcast(FP8X4), scales=w2_scales[s][:], in_=w2_bf[s][:])
-
-        jobs = []
-        for u, (g, lo, hi) in enumerate(PIECES):
-            per_bank = BANK // (hi - lo)
-            jobs.extend((u, t0, per_bank) for t0 in range(0, PACK, per_bank))
-        bank_of = {}
-        count = [0, 0]
-        for job in jobs:
-            c = PIECES[job[0]][0] % 2
-            bank_of[job] = (c, count[c] % Z_BANKS)
-            count[c] = count[c] + 1
-        filled = []
-        emptied = []
-
-        def x_part(s, n0):
-            return [i for i, (ss, lo, hi) in enumerate(X_PARTS) if ss == s and lo <= n0 < hi][0]
-
-        def ready(job):
-            g, lo, hi = PIECES[job[0]]
-            s = g // 2
-            return (
-                all(i in w1_done for i, part in enumerate(W1_PARTS) if part[0] == s)
-                and all(x_part(s, n0) in x_done for n0 in range(lo, hi, NMM))
-                and all(other in emptied for other in filled if bank_of[other] == bank_of[job])
-            )
-
-        def fill_banks():
-            blocked = set()
-            for job in jobs:
-                c = bank_of[job][0]
-                if job in filled or c in blocked:
-                    continue
-                if not ready(job):
-                    blocked.add(c)
-                    continue
-                first_product(job)
-                filled.append(job)
-
-        def first_product(job):
-            u, t0, places = job
-            g, lo, hi = PIECES[u]
-            s, c = divmod(g, 2)
-            rows = slice(c * ROWS, (c + 1) * ROWS)
-            bank = z_banks[c][bank_of[job][1]]
-            for e in range(places):
-                codes, scales = w1_operand(s, t0 + e)
-                for n0 in range(lo, hi, NMM):
-                    i = x_part(s, n0)
-                    cols = slice(n0 - X_PARTS[i][1], n0 - X_PARTS[i][1] + NMM)
-                    at = e * (hi - lo) + n0 - lo
-                    nc.tensor.matmul_mx(
-                        out=bank[:, at : at + NMM],
-                        lhsT=codes[rows, :].bitcast(FP8X4),
-                        lhsT_scale=scales[rows, :],
-                        rhs=x_codes[i][rows, cols].bitcast(FP8X4),
-                        rhs_scale=x_scales[i][rows, cols],
-                        start=True,
-                        stop=True,
-                    )
-
-        def sigmoid(u):
-            g, lo, hi = PIECES[u]
-            for job in jobs:
-                if job[0] != u:
-                    continue
-                assert job in filled
-                c, i = bank_of[job]
-                for e in range(job[2]):
-                    t = job[1] + e
-                    nc.scalar.activation(
-                        out=sig[u][:, t, :],
-                        in_=z_banks[c][i][:, e * (hi - lo) : (e + 1) * (hi - lo)],
-                        func=SIGMOID,
-                        bias=vec_turned[:, 32 * t + 8 * g : 32 * t + 8 * g + 1],
-                    )
-                emptied.append(job)
-                fill_banks()
-
-        def scale_h(u):
-            g, lo, hi = PIECES[u]
-            nc.vector.tensor_tensor(
-                out=h_bf[u][:].rearrange("p (c i t) -> p c t i", i=HRUN, t=PACK),
-                in0=sig[u][:].rearrange("p t (c i) -> p c t i", i=HRUN),
-                in1=gain[:, g, 0:PACK].unsqueeze(1).unsqueeze(3).to_broadcast([P, (hi - lo) // HRUN, PACK, HRUN]),
-                op=MULT,
-            )
-
-        def scale_h_on_scalar(u):
-            g, lo, hi = PIECES[u]
-            for t in range(PACK):
-                nc.scalar.activation(out=h_pl[u][:, t, :], in_=sig[u][:, t, :], func=COPY, scale=gain[:, g, t : t + 1])
-
-        def weave_h(engine, u):
-            copy(
-                engine,
-                h_bf[u][:].rearrange("p (c i t) -> p c t i", i=RUN, t=PACK),
-                h_pl[u][:].rearrange("p t (c i) -> p c t i", i=RUN),
-            )
-
-        def quant_h(u):
-            nc.vector.quantize_mx(out=h_codes[u][:].bitcast(FP8X4), scales=h_scales[u][:], in_=h_bf[u][:])
-
-        def second_product(u):
-            g, lo, hi = PIECES[u]
-            s, c = divmod(g, 2)
-            o = [k for k, (gg, l0, l1) in enumerate(OUTS) if gg == g and l0 <= lo < l1][0]
-            at = lo - OUTS[o][1]
-            for n0 in range(0, hi - lo, NMM):
-                nc.tensor.matmul_mx(
-                    out=y_banks[o % 2][:, at + n0 : at + n0 + NMM],
-                    lhsT=w2_codes[s][:, c * M : (c + 1) * M].bitcast(FP8X4),
-                    lhsT_scale=w2_scales[s][:, c * M : (c + 1) * M],
-                    rhs=h_codes[u][:, n0 : n0 + NMM].bitcast(FP8X4),
-                    rhs_scale=h_scales[u][:, n0 : n0 + NMM],
-                    start=True,
-                    stop=True,
-                )
-
-        def finish(o, queue=nc.sync):
-            g, lo, hi = OUTS[o]
-            nc.vector.tensor_tensor(out=y_sb[o][:], in0=y_banks[o % 2][:, 0 : hi - lo], in1=r_sb[g][:, lo:hi], op=ADD)
-            queue.dma_start(out=out[g][:, lo:hi], in_=y_sb[o][:])
 
         def load_vectors():
             for v, src in enumerate((b, hs)):
@@ -301,95 +99,223 @@ def tile_rows_gmlp_sigmoid_bias_res_kernel(tc, x, w1, hs, w2, b, r, out):
 
         def gather_gain():
             nc.vector.tensor_copy(
-                out=gain[:, :, 0:PACK],
+                out=gain[:],
                 in_=vec_turned[:, P : 2 * P].rearrange("p (t g z) -> p g t z", t=PACK, g=G)[:, :, :, 0],
             )
 
+        def copy(engine, dst, src):
+            if engine == "V":
+                nc.vector.tensor_copy(out=dst, in_=src)
+            else:
+                nc.scalar.copy(out=dst, in_=src)
+
+        def round_w1(engine, s, u, a=0, z=P):
+            copy(
+                engine,
+                w1_bf[s][u][:].rearrange("p (e m j) -> p m j e", e=2, j=PACK)[:, a:z],
+                w1_raw[s][:].rearrange("p j (m u e) -> p u m j e", u=2, e=2)[:, u, a:z],
+            )
+
+        def quant_w1(s, t):
+            u, e = divmod(t, 2)
+            nc.vector.quantize_mx(
+                out=w1_codes[s][t][:].bitcast(FP8X4),
+                scales=w1_scales[s][t][:],
+                in_=w1_bf[s][u][:, e * PACK * P : (e + 1) * PACK * P],
+            )
+
+        def round_x(engine, s, lo, hi):
+            copy(
+                engine,
+                x_bf[s][:, PACK * lo : PACK * hi].rearrange("p (c i j) -> p c j i", i=RUN, j=PACK),
+                x_raw[s][:, :, lo:hi].rearrange("p j (c i) -> p c j i", i=RUN),
+            )
+
+        def quant_x(s):
+            nc.vector.quantize_mx(out=x_codes[s][:].bitcast(FP8X4), scales=x_scales[s][:], in_=x_bf[s][:])
+
+        def round_w2(engine, g):
+            copy(
+                engine,
+                w2_bf[g][:].rearrange("p (c i j) -> p c j i", i=RUN, j=PACK),
+                w2_raw[g // 2][:, g % 2].rearrange("p j (c i) -> p c j i", i=RUN),
+            )
+
+        def quant_w2(g):
+            nc.vector.quantize_mx(out=w2_codes[g][:].bitcast(FP8X4), scales=w2_scales[g][:], in_=w2_bf[g][:])
+
+        def z_bank(g, t):
+            return z_banks[g % 2][(PACK * (g // 2) + t) % Z_BANKS]
+
+        def first_product(g, t):
+            s, c = divmod(g, 2)
+            rows = slice(c * ROWS, (c + 1) * ROWS)
+            nc.tensor.matmul_mx(
+                out=z_bank(g, t)[:],
+                lhsT=w1_codes[s][t][rows, :].bitcast(FP8X4),
+                lhsT_scale=w1_scales[s][t][rows, :],
+                rhs=x_codes[s][rows, :].bitcast(FP8X4),
+                rhs_scale=x_scales[s][rows, :],
+                start=True,
+                stop=True,
+            )
+
+        def sigmoid(g, t, a=None):
+            w = WIDTH[g]
+            src = z_bank(g, t)[:].rearrange("p (a w) -> p a w", w=w)
+            nc.scalar.activation(
+                out=sig[g][:, :, t, :] if a is None else sig[g][:, a, t, :],
+                in_=src if a is None else src[:, a, :],
+                func=SIGMOID,
+                bias=vec_turned[:, 32 * t + 8 * g : 32 * t + 8 * g + 1],
+            )
+
+        def scale_h(g, a):
+            nc.vector.tensor_tensor(
+                out=h_bf[g][a][:].rearrange("p (c i t) -> p c t i", i=HRUN, t=PACK),
+                in0=sig[g][:, a].rearrange("p t (c i) -> p c t i", i=HRUN),
+                in1=gain[:, g, :].unsqueeze(1).unsqueeze(3).to_broadcast([P, WIDTH[g] // HRUN, PACK, HRUN]),
+                op=MULT,
+            )
+
+        def scale_h_on_scalar(g, a):
+            for t in range(PACK):
+                nc.scalar.activation(out=h_rows[g, a][:, t, :], in_=sig[g][:, a, t, :], func=COPY, scale=gain[:, g, t : t + 1])
+
+        def weave_h(engine, g, a):
+            copy(
+                engine,
+                h_bf[g][a][:].rearrange("p (c i t) -> p c t i", i=RUN, t=PACK),
+                h_rows[g, a][:].rearrange("p t (c i) -> p c t i", i=RUN),
+            )
+
+        def quant_h(g, a):
+            cols = slice(a * WIDTH[g], (a + 1) * WIDTH[g])
+            nc.vector.quantize_mx(out=h_codes[g][:, cols].bitcast(FP8X4), scales=h_scales[g][:, cols], in_=h_bf[g][a][:])
+
+        def second_product(g):
+            nc.tensor.matmul_mx(
+                out=y_banks[g % 2][:],
+                lhsT=w2_codes[g][:].bitcast(FP8X4),
+                lhsT_scale=w2_scales[g][:],
+                rhs=h_codes[g][:].bitcast(FP8X4),
+                rhs_scale=h_scales[g][:],
+                start=True,
+                stop=True,
+            )
+
+        def finish(g, lo=0, hi=N, queue=nc.sync):
+            nc.vector.tensor_tensor(out=y_sb[g, lo][:, lo:hi], in0=y_banks[g % 2][:, lo:hi], in1=r_sb[g][:, lo:hi], op=ADD)
+            queue.dma_start(out=out[g][:, lo:hi], in_=y_sb[g, lo][:, lo:hi])
+
         def warm_up():
-            nc.vector.memset(warm[:, 0:8], 0.0)
             nc.vector.memset(vec_rows[:], 0.0)
-            nc.scalar.activation(out=warm[:, 8:9], in_=warm[:, 0:1], func=SIGMOID)
 
         warm_up()
-        load_w1(0)
-        load_vectors()
         load_x(0)
+        load_vectors()
+        load_w1(0)
         load_x(1)
         load_w1(1)
-        load_x(2)
         load_w2(0)
         load_r(0)
         load_w2(1)
         load_r(1)
         load_r(2)
         load_r(3)
-        round_w1("V", 0, 0, 80)
-        round_w1("S", 0, 80, 128)
+        round_x("V", 0, 0, 512)
         deal_vectors()
-        quant_w1(0)
-        round_x("V", 0)
-        round_x("S", 1)
-        turn_vectors()
         quant_x(0)
-        quant_x(1)
+        round_w1("V", 0, 0)
+        turn_vectors()
+        quant_w1(0, 0)
+        first_product(0, 0)
+        quant_w1(0, 1)
+        first_product(0, 1)
+        round_w1("V", 0, 1)
         gather_gain()
-        round_x("V", 2)
-        sigmoid(0)
-        sigmoid(1)
-        scale_h(0)
-        quant_x(2)
-        scale_h(1)
-        quant_h(0)
-        sigmoid(2)
-        round_w1("V", 1, 0, 64)
-        round_w1("S", 1, 64, 128)
-        quant_h(1)
-        scale_h(2)
-        quant_w1(1)
-        sigmoid(3)
-        quant_h(2)
-        round_x("S", 3)
-        scale_h(3)
-        quant_x(3)
-        sigmoid(4)
-        quant_h(3)
-        round_w2("V", 0)
-        scale_h(4)
+        quant_w1(0, 2)
+        first_product(0, 2)
+        quant_w1(0, 3)
+        sigmoid(0, 0)
+        first_product(0, 3)
+        first_product(1, 0)
+        first_product(1, 1)
+        first_product(1, 2)
+        sigmoid(0, 1)
+        sigmoid(0, 2)
+        sigmoid(0, 3, 0)
+        sigmoid(0, 3, 1)
+        round_x("V", 1, 0, 512)
+        quant_x(1)
+        scale_h(0, 0)
+        sigmoid(1, 0)
+        first_product(1, 3)
+        round_w1("S", 1, 0)
+        round_w1("V", 1, 1)
+        quant_h(0, 0)
+        quant_w1(1, 0)
+        first_product(2, 0)
+        quant_w1(1, 1)
+        first_product(2, 1)
+        quant_w1(1, 2)
+        first_product(2, 2)
+        quant_w1(1, 3)
+        scale_h(0, 1)
+        sigmoid(1, 1)
+        sigmoid(1, 2)
+        sigmoid(1, 3, 0)
+        sigmoid(1, 3, 1)
+        first_product(3, 0)
+        round_w2("S", 0)
+        sigmoid(2, 0)
+        first_product(2, 3)
+        first_product(3, 1)
+        scale_h(1, 0)
+        quant_h(0, 1)
         quant_w2(0)
-        sigmoid(5)
         second_product(0)
-        second_product(1)
-        second_product(3)
-        quant_h(4)
-        round_x("S", 4)
-        second_product(2)
-        second_product(4)
-        scale_h(5)
-        quant_x(4)
-        sigmoid(6)
-        finish(0)
-        quant_h(5)
+        first_product(3, 2)
+        scale_h(1, 1)
+        quant_h(1, 0)
+        sigmoid(2, 1)
+        sigmoid(2, 2)
+        sigmoid(2, 3, 0)
+        sigmoid(2, 3, 1)
         round_w2("S", 1)
-        scale_h(6)
+        quant_h(1, 1)
+        scale_h(2, 0)
+        finish(0)
         quant_w2(1)
-        sigmoid(7)
-        second_product(5)
+        sigmoid(3, 0)
+        first_product(3, 3)
+        second_product(1)
+        round_w2("S", 2)
+        scale_h(2, 1)
+        quant_h(2, 0)
         finish(1)
-        quant_h(6)
-        second_product(6)
+        sigmoid(3, 1)
+        sigmoid(3, 2)
+        sigmoid(3, 3, 0)
+        sigmoid(3, 3, 1)
+        sigmoid(3, 3, 2)
+        sigmoid(3, 3, 3)
+        round_w2("S", 3)
+        scale_h_on_scalar(3, 3)
+        scale_h_on_scalar(3, 2)
+        weave_h("S", 3, 3)
+        weave_h("S", 3, 2)
+        quant_h(2, 1)
+        quant_w2(2)
+        second_product(2)
+        scale_h(3, 0)
+        scale_h(3, 1)
+        quant_h(3, 0)
+        quant_w2(3)
+        quant_h(3, 1)
+        quant_h(3, 3)
+        quant_h(3, 2)
+        second_product(3)
         finish(2)
-        scale_h(7)
-        sigmoid(8)
-        sigmoid(9)
-        scale_h_on_scalar(9)
-        weave_h("S", 9)
-        finish(3)
-        quant_h(7)
-        second_product(7)
-        scale_h(8)
-        finish(4)
-        quant_h(8)
-        second_product(8)
-        quant_h(9)
-        second_product(9)
-        finish(5)
+        finish(3, 0, 256)
+        finish(3, 256, 512)

@@ -19,11 +19,12 @@ P = 128
 PACK = 4
 ROWS = 64
 PAIRS = 2
-HALF = N // 2
 RUN = 2
-HRUN = 2
-Z_BANKS = 3
-WIDTH = [256, 256, 256, 128]
+NMM = 128
+Z_BANKS = (3, 2)
+X_PIECES = [[(0, 128), (128, 256), (256, 512)], [(0, 512)]]
+W1_PIECES = [[(0, 2), (2, 4)], [(0, 4)]]
+SIG_TILES = [[(0, 128, 128), (128, 256, 128), (256, 512, 256)]] * 2 + [[(0, 256, 256), (256, 512, 256)], [(0, 256, 256), (256, 512, 128)]]
 
 
 def tile_rows_gmlp_sigmoid_bias_res_kernel(tc, x, w1, hs, w2, b, r, out):
@@ -36,42 +37,46 @@ def tile_rows_gmlp_sigmoid_bias_res_kernel(tc, x, w1, hs, w2, b, r, out):
         def tile(name, shape, dtype):
             return sb.tile(shape, dtype, name=name, align_bytes=64)
 
-        w1_raw = [tile("w1_raw%d" % s, [P, PACK, K], F32) for s in range(PAIRS)]
+        w1_raw = {(s, lo): tile("w1_raw%d_%d" % (s, lo), [P, hi - lo, K], F32) for s in range(PAIRS) for lo, hi in W1_PIECES[s]}
         w1_bf = [[tile("w1_bf%d%d" % (s, u), [P, 2 * PACK * P], BF16) for u in range(2)] for s in range(PAIRS)]
         w1_codes = [[tile("w1_codes%d%d" % (s, t), [P, P], U32) for t in range(PACK)] for s in range(PAIRS)]
         w1_scales = [[tile("w1_scales%d%d" % (s, t), [P, P], U8) for t in range(PACK)] for s in range(PAIRS)]
-        x_raw = [tile("x_raw%d" % s, [P, PACK, N], F32) for s in range(PAIRS)]
+        x_raw = {(s, lo): tile("x_raw%d_%d" % (s, lo), [P, PACK, hi - lo], F32) for s in range(PAIRS) for lo, hi in X_PIECES[s]}
         x_bf = [tile("x_bf%d" % s, [P, PACK * N], BF16) for s in range(PAIRS)]
         x_codes = [tile("x_codes%d" % s, [P, N], U32) for s in range(PAIRS)]
         x_scales = [tile("x_scales%d" % s, [P, N], U8) for s in range(PAIRS)]
         w2_raw = [tile("w2_raw%d" % s, [P, 2, PACK, M], F32) for s in range(PAIRS)]
-        w2_bf = [tile("w2_bf%d" % g, [P, PACK * M], BF16) for g in range(G)]
-        w2_codes = [tile("w2_codes%d" % g, [P, M], U32) for g in range(G)]
-        w2_scales = [tile("w2_scales%d" % g, [P, M], U8) for g in range(G)]
+        w2_bf = [tile("w2_bf%d" % s, [P, 2 * PACK * M], BF16) for s in range(PAIRS)]
+        w2_codes = [tile("w2_codes%d" % s, [P, 2 * M], U32) for s in range(PAIRS)]
+        w2_scales = [tile("w2_scales%d" % s, [P, 2 * M], U8) for s in range(PAIRS)]
         r_sb = [tile("r_sb%d" % g, [P, N], F32) for g in range(G)]
-        vec_rows = tile("vec_rows", [P, 2 * P], F32)
-        vec_dealt = tile("vec_dealt", [P, 2 * P], F32)
-        vec_turned = tile("vec_turned", [P, 2 * P], F32)
+        vec_rows = tile("vec_rows", [P, P], F32)
+        vec_dealt = tile("vec_dealt", [P, P], F32)
+        vec_turned = tile("vec_turned", [P, P], F32)
         gain = tile("gain", [P, G, PACK], F32)
 
-        sig = [tile("sig%d" % g, [P, N // WIDTH[g], PACK, WIDTH[g]], F32) for g in range(G)]
-        h_rows = {(g, a): tile("h_rows%d%d" % (g, a), [P, PACK, WIDTH[g]], BF16) for g in range(G) for a in range(N // WIDTH[g])}
-        h_bf = [[tile("h_bf%d%d" % (g, a), [P, PACK * WIDTH[g]], BF16) for a in range(N // WIDTH[g])] for g in range(G)]
+        sig = {(g, lo): tile("sig%d_%d" % (g, lo), [P, (hi - lo) // w, PACK, w], F32) for g in range(G) for lo, hi, w in SIG_TILES[g]}
+        h_rows = {}
+        h_bf = [tile("h_bf%d" % g, [P, PACK * N], BF16) for g in range(G)]
         h_codes = [tile("h_codes%d" % g, [P, N], U32) for g in range(G)]
         h_scales = [tile("h_scales%d" % g, [P, N], U8) for g in range(G)]
-        y_sb = {(g, lo): tile("y_sb%d_%d" % (g, lo), [P, N], F32) for g in range(G) for lo in (0, 128, 256, 384)}
+        y_sb = [tile("y_sb%d" % g, [P, N], F32) for g in range(G)]
 
-        z_banks = [[ps.tile([P, N], F32, name="z%d%d" % (c, i)) for i in range(Z_BANKS)] for c in range(2)]
-        y_banks = [ps.tile([P, N], F32, name="y%d" % i) for i in range(2)]
+        z_banks = [[ps.tile([P, N], F32, name="z%d%d" % (c, i)) for i in range(Z_BANKS[c])] for c in range(2)]
+        y_banks = [ps.tile([P, N], F32, name="y%d" % i) for i in range(3)]
+        z_turn = [0, 0]
+        z_place = {}
 
         def pair(t, s):
             return t[2 * s : 2 * s + 2].rearrange("g (p j) n -> (g p) j n", j=PACK)
 
-        def load_w1(s):
-            nc.sync.dma_start(out=w1_raw[s][:], in_=pair(w1, s))
+        def load_w1(s, i):
+            lo, hi = W1_PIECES[s][i]
+            nc.sync.dma_start(out=w1_raw[s, lo][:], in_=pair(w1, s)[:, lo:hi, :])
 
-        def load_x(s):
-            nc.sync.dma_start(out=x_raw[s][:], in_=pair(x, s))
+        def load_x(s, i):
+            lo, hi = X_PIECES[s][i]
+            nc.sync.dma_start(out=x_raw[s, lo][:], in_=pair(x, s)[:, :, lo:hi])
 
         def load_w2(s):
             nc.sync.dma_start(
@@ -84,24 +89,22 @@ def tile_rows_gmlp_sigmoid_bias_res_kernel(tc, x, w1, hs, w2, b, r, out):
 
         def load_vectors():
             for v, src in enumerate((b, hs)):
-                nc.sync.dma_start(
-                    out=vec_rows[0:P:8, v * P : (v + 1) * P], in_=src.rearrange("g (q a) o -> q g (a o)", q=4)
-                )
+                nc.sync.dma_start(out=vec_rows[4 * v : P : 8, :], in_=src.rearrange("g (q a) o -> q g (a o)", q=4))
+
+        def clear_vectors():
+            nc.vector.memset(vec_rows[:], 0.0)
 
         def deal_vectors():
             nc.vector.tensor_copy(
-                out=vec_dealt[:].rearrange("p (v t s) -> p v t s", v=2, t=PACK),
-                in_=vec_rows[:].rearrange("p (v s t) -> p v t s", v=2, t=PACK),
+                out=vec_dealt[:].rearrange("p (t s) -> p t s", t=PACK),
+                in_=vec_rows[:].rearrange("p (s t) -> p t s", t=PACK),
             )
 
         def turn_vectors():
             nc.vector.transpose(out=vec_turned[:], in_=vec_dealt[:])
 
         def gather_gain():
-            nc.vector.tensor_copy(
-                out=gain[:],
-                in_=vec_turned[:, P : 2 * P].rearrange("p (t g z) -> p g t z", t=PACK, g=G)[:, :, :, 0],
-            )
+            nc.vector.tensor_copy(out=gain[:], in_=vec_turned[:].rearrange("p (t g z) -> p g t z", t=PACK, g=G)[:, :, :, 4])
 
         def copy(engine, dst, src):
             if engine == "V":
@@ -109,11 +112,12 @@ def tile_rows_gmlp_sigmoid_bias_res_kernel(tc, x, w1, hs, w2, b, r, out):
             else:
                 nc.scalar.copy(out=dst, in_=src)
 
-        def round_w1(engine, s, u, a=0, z=P):
+        def round_w1(engine, s, u, i=0, a=0, z=P):
+            lo, hi = W1_PIECES[s][i]
             copy(
                 engine,
-                w1_bf[s][u][:].rearrange("p (e m j) -> p m j e", e=2, j=PACK)[:, a:z],
-                w1_raw[s][:].rearrange("p j (m u e) -> p u m j e", u=2, e=2)[:, u, a:z],
+                w1_bf[s][u][:].rearrange("p (e m j) -> p m j e", e=2, j=PACK)[:, a:z, lo:hi],
+                w1_raw[s, lo][:].rearrange("p j (m u e) -> p u m j e", u=2, e=2)[:, u, a:z],
             )
 
         def quant_w1(s, t):
@@ -125,197 +129,232 @@ def tile_rows_gmlp_sigmoid_bias_res_kernel(tc, x, w1, hs, w2, b, r, out):
             )
 
         def round_x(engine, s, lo, hi):
+            start = max(a for a, z in X_PIECES[s] if a <= lo)
             copy(
                 engine,
                 x_bf[s][:, PACK * lo : PACK * hi].rearrange("p (c i j) -> p c j i", i=RUN, j=PACK),
-                x_raw[s][:, :, lo:hi].rearrange("p j (c i) -> p c j i", i=RUN),
+                x_raw[s, start][:, :, lo - start : hi - start].rearrange("p j (c i) -> p c j i", i=RUN),
             )
 
-        def quant_x(s):
-            nc.vector.quantize_mx(out=x_codes[s][:].bitcast(FP8X4), scales=x_scales[s][:], in_=x_bf[s][:])
+        def quant_x(s, lo, hi):
+            nc.vector.quantize_mx(
+                out=x_codes[s][:, lo:hi].bitcast(FP8X4), scales=x_scales[s][:, lo:hi], in_=x_bf[s][:, PACK * lo : PACK * hi]
+            )
 
-        def round_w2(engine, g):
+        def round_w2(engine, g, count=1):
+            s, c = divmod(g, 2)
             copy(
                 engine,
-                w2_bf[g][:].rearrange("p (c i j) -> p c j i", i=RUN, j=PACK),
-                w2_raw[g // 2][:, g % 2].rearrange("p j (c i) -> p c j i", i=RUN),
+                w2_bf[s][:, c * PACK * M : (c + count) * PACK * M].rearrange("p (g c i j) -> p g c j i", g=count, i=RUN, j=PACK),
+                w2_raw[s][:, c : c + count].rearrange("p g j (c i) -> p g c j i", i=RUN),
             )
 
-        def quant_w2(g):
-            nc.vector.quantize_mx(out=w2_codes[g][:].bitcast(FP8X4), scales=w2_scales[g][:], in_=w2_bf[g][:])
+        def quant_w2(g, count=1):
+            s, c = divmod(g, 2)
+            nc.vector.quantize_mx(
+                out=w2_codes[s][:, c * M : (c + count) * M].bitcast(FP8X4),
+                scales=w2_scales[s][:, c * M : (c + count) * M],
+                in_=w2_bf[s][:, c * PACK * M : (c + count) * PACK * M],
+            )
 
-        def z_bank(g, t):
-            return z_banks[g % 2][(PACK * (g // 2) + t) % Z_BANKS]
-
-        def first_product(g, t):
+        def first_product(g, places, lo, hi):
             s, c = divmod(g, 2)
             rows = slice(c * ROWS, (c + 1) * ROWS)
-            nc.tensor.matmul_mx(
-                out=z_bank(g, t)[:],
-                lhsT=w1_codes[s][t][rows, :].bitcast(FP8X4),
-                lhsT_scale=w1_scales[s][t][rows, :],
-                rhs=x_codes[s][rows, :].bitcast(FP8X4),
-                rhs_scale=x_scales[s][rows, :],
-                start=True,
-                stop=True,
-            )
+            bank = z_banks[c][z_turn[c] % Z_BANKS[c]]
+            z_turn[c] = z_turn[c] + 1
+            for n, t in enumerate(places):
+                base = n * (hi - lo) - lo
+                for col in range(lo, hi, NMM):
+                    z_place[g, t, col] = (bank, base)
+                    nc.tensor.matmul_mx(
+                        out=bank[:, base + col : base + col + NMM],
+                        lhsT=w1_codes[s][t][rows, :].bitcast(FP8X4),
+                        lhsT_scale=w1_scales[s][t][rows, :],
+                        rhs=x_codes[s][rows, col : col + NMM].bitcast(FP8X4),
+                        rhs_scale=x_scales[s][rows, col : col + NMM],
+                        start=True,
+                        stop=True,
+                    )
 
-        def sigmoid(g, t, a=None):
-            w = WIDTH[g]
-            src = z_bank(g, t)[:].rearrange("p (a w) -> p a w", w=w)
+        def sig_tile(g, lo):
+            return max((start, w) for start, end, w in SIG_TILES[g] if start <= lo)
+
+        def sig_part(g, lo, hi):
+            start, w = sig_tile(g, lo)
+            assert hi - lo == w
+            return sig[g, start][:, (lo - start) // w]
+
+        def sigmoid(g, t, lo, hi):
+            bank, base = z_place[g, t, lo]
+            start, w = sig_tile(g, lo)
             nc.scalar.activation(
-                out=sig[g][:, :, t, :] if a is None else sig[g][:, a, t, :],
-                in_=src if a is None else src[:, a, :],
+                out=sig[g, start][:, (lo - start) // w : (hi - start) // w, t, :],
+                in_=bank[:, base + lo : base + hi].rearrange("p (a w) -> p a w", w=w),
                 func=SIGMOID,
                 bias=vec_turned[:, 32 * t + 8 * g : 32 * t + 8 * g + 1],
             )
 
-        def scale_h(g, a):
+        def scale_h(g, lo, hi):
             nc.vector.tensor_tensor(
-                out=h_bf[g][a][:].rearrange("p (c i t) -> p c t i", i=HRUN, t=PACK),
-                in0=sig[g][:, a].rearrange("p t (c i) -> p c t i", i=HRUN),
-                in1=gain[:, g, :].unsqueeze(1).unsqueeze(3).to_broadcast([P, WIDTH[g] // HRUN, PACK, HRUN]),
+                out=h_bf[g][:, PACK * lo : PACK * hi].rearrange("p (c i t) -> p c t i", i=RUN, t=PACK),
+                in0=sig_part(g, lo, hi).rearrange("p t (c i) -> p c t i", i=RUN),
+                in1=gain[:, g, :].unsqueeze(1).unsqueeze(3).to_broadcast([P, (hi - lo) // RUN, PACK, RUN]),
                 op=MULT,
             )
 
-        def scale_h_on_scalar(g, a):
-            for t in range(PACK):
-                nc.scalar.activation(out=h_rows[g, a][:, t, :], in_=sig[g][:, a, t, :], func=COPY, scale=gain[:, g, t : t + 1])
+        def scale_h_on_scalar(g, lo, hi, places=range(PACK)):
+            if (g, lo) not in h_rows:
+                h_rows[g, lo] = tile("h_rows%d_%d" % (g, lo), [P, PACK, hi - lo], BF16)
+            for t in places:
+                nc.scalar.activation(out=h_rows[g, lo][:, t, :], in_=sig_part(g, lo, hi)[:, t, :], func=COPY, scale=gain[:, g, t : t + 1])
 
-        def weave_h(engine, g, a):
+        def weave_h(engine, g, lo, hi, start=None):
+            start = lo if start is None else start
             copy(
                 engine,
-                h_bf[g][a][:].rearrange("p (c i t) -> p c t i", i=RUN, t=PACK),
-                h_rows[g, a][:].rearrange("p t (c i) -> p c t i", i=RUN),
+                h_bf[g][:, PACK * lo : PACK * hi].rearrange("p (c i t) -> p c t i", i=RUN, t=PACK),
+                h_rows[g, start][:, :, lo - start : hi - start].rearrange("p t (c i) -> p c t i", i=RUN),
             )
 
-        def quant_h(g, a):
-            cols = slice(a * WIDTH[g], (a + 1) * WIDTH[g])
-            nc.vector.quantize_mx(out=h_codes[g][:, cols].bitcast(FP8X4), scales=h_scales[g][:, cols], in_=h_bf[g][a][:])
-
-        def second_product(g):
-            nc.tensor.matmul_mx(
-                out=y_banks[g % 2][:],
-                lhsT=w2_codes[g][:].bitcast(FP8X4),
-                lhsT_scale=w2_scales[g][:],
-                rhs=h_codes[g][:].bitcast(FP8X4),
-                rhs_scale=h_scales[g][:],
-                start=True,
-                stop=True,
+        def quant_h(g, lo, hi):
+            nc.vector.quantize_mx(
+                out=h_codes[g][:, lo:hi].bitcast(FP8X4), scales=h_scales[g][:, lo:hi], in_=h_bf[g][:, PACK * lo : PACK * hi]
             )
 
-        def finish(g, lo=0, hi=N, queue=nc.sync):
-            nc.vector.tensor_tensor(out=y_sb[g, lo][:, lo:hi], in0=y_banks[g % 2][:, lo:hi], in1=r_sb[g][:, lo:hi], op=ADD)
-            queue.dma_start(out=out[g][:, lo:hi], in_=y_sb[g, lo][:, lo:hi])
+        def second_product(g, lo, hi, bank):
+            s, c = divmod(g, 2)
+            for col in range(lo, hi, NMM):
+                nc.tensor.matmul_mx(
+                    out=y_banks[bank][:, col : col + NMM],
+                    lhsT=w2_codes[s][:, c * M : (c + 1) * M].bitcast(FP8X4),
+                    lhsT_scale=w2_scales[s][:, c * M : (c + 1) * M],
+                    rhs=h_codes[g][:, col : col + NMM].bitcast(FP8X4),
+                    rhs_scale=h_scales[g][:, col : col + NMM],
+                    start=True,
+                    stop=True,
+                )
 
-        def warm_up():
-            nc.vector.memset(vec_rows[:], 0.0)
+        def finish(g, lo, hi, bank):
+            nc.vector.tensor_tensor(out=y_sb[g][:, lo:hi], in0=y_banks[bank][:, lo:hi], in1=r_sb[g][:, lo:hi], op=ADD)
+            nc.sync.dma_start(out=out[g][:, lo:hi], in_=y_sb[g][:, lo:hi])
 
-        warm_up()
-        load_x(0)
+        clear_vectors()
+        load_x(0, 0)
         load_vectors()
-        load_w1(0)
-        load_x(1)
-        load_w1(1)
+        load_w1(0, 0)
+        load_w1(0, 1)
+        load_x(0, 1)
+        load_x(0, 2)
+        load_w1(1, 0)
+        load_x(1, 0)
         load_w2(0)
         load_r(0)
-        load_w2(1)
         load_r(1)
+        load_w2(1)
         load_r(2)
         load_r(3)
-        round_x("V", 0, 0, 512)
+        round_x("V", 0, 0, 128)
         deal_vectors()
-        quant_x(0)
-        round_w1("V", 0, 0)
+        quant_x(0, 0, 128)
         turn_vectors()
-        quant_w1(0, 0)
-        first_product(0, 0)
-        quant_w1(0, 1)
-        first_product(0, 1)
-        round_w1("V", 0, 1)
+        round_w1("V", 0, 0, 0)
         gather_gain()
-        quant_w1(0, 2)
-        first_product(0, 2)
-        quant_w1(0, 3)
-        sigmoid(0, 0)
-        first_product(0, 3)
-        first_product(1, 0)
-        first_product(1, 1)
-        first_product(1, 2)
-        sigmoid(0, 1)
-        sigmoid(0, 2)
-        sigmoid(0, 3, 0)
-        sigmoid(0, 3, 1)
-        round_x("V", 1, 0, 512)
-        quant_x(1)
-        scale_h(0, 0)
-        sigmoid(1, 0)
-        first_product(1, 3)
-        round_w1("S", 1, 0)
-        round_w1("V", 1, 1)
-        quant_h(0, 0)
-        quant_w1(1, 0)
-        first_product(2, 0)
-        quant_w1(1, 1)
-        first_product(2, 1)
-        quant_w1(1, 2)
-        first_product(2, 2)
-        quant_w1(1, 3)
-        scale_h(0, 1)
-        sigmoid(1, 1)
-        sigmoid(1, 2)
-        sigmoid(1, 3, 0)
-        sigmoid(1, 3, 1)
-        first_product(3, 0)
+        round_w1("V", 0, 1, 0)
+        round_w1("V", 0, 0, 1)
+        round_w1("V", 0, 1, 1)
+        for t in range(4):
+            quant_w1(0, t)
+        first_product(0, [0], 0, 128)
+        first_product(0, [1], 0, 128)
+        first_product(0, [2, 3], 0, 128)
+        first_product(1, [0, 1], 0, 128)
+        first_product(1, [2, 3], 0, 128)
+        round_x("V", 0, 128, 256)
+        for t in range(4):
+            sigmoid(0, t, 0, 128)
+        quant_x(0, 128, 256)
+        first_product(0, [0, 1, 2, 3], 128, 256)
+        for t in range(4):
+            sigmoid(1, t, 0, 128)
+        first_product(1, [0, 1, 2, 3], 128, 256)
+        round_x("V", 0, 256, 512)
+        scale_h(0, 0, 128)
+        quant_x(0, 256, 512)
+        first_product(0, [0, 1], 256, 512)
+        first_product(0, [2, 3], 256, 512)
+        first_product(1, [0, 1], 256, 512)
+        for t in range(4):
+            sigmoid(0, t, 128, 256)
+        for t in range(4):
+            sigmoid(1, t, 128, 256)
+        first_product(1, [2, 3], 256, 512)
+        scale_h(1, 0, 128)
+        scale_h(0, 128, 256)
+        for t in range(4):
+            sigmoid(0, t, 256, 512)
+        round_w1("S", 1, 1)
+        round_x("S", 1, 256, 512)
+        for t in range(4):
+            sigmoid(1, t, 256, 512)
+        round_w1("V", 1, 0)
+        scale_h(1, 128, 256)
+        quant_h(0, 0, 256)
+        quant_h(1, 0, 256)
+        round_x("V", 1, 0, 256)
+        for t in range(4):
+            quant_w1(1, t)
+        quant_x(1, 0, 256)
+        first_product(2, [0, 1], 0, 256)
+        first_product(2, [2, 3], 0, 256)
         round_w2("S", 0)
-        sigmoid(2, 0)
-        first_product(2, 3)
-        first_product(3, 1)
-        scale_h(1, 0)
-        quant_h(0, 1)
+        scale_h(0, 256, 512)
+        quant_x(1, 256, 512)
+        first_product(2, [0, 1], 256, 512)
+        scale_h(1, 256, 512)
+        quant_h(0, 256, 512)
         quant_w2(0)
-        second_product(0)
-        first_product(3, 2)
-        scale_h(1, 1)
-        quant_h(1, 0)
-        sigmoid(2, 1)
-        sigmoid(2, 2)
-        sigmoid(2, 3, 0)
-        sigmoid(2, 3, 1)
+        quant_h(1, 256, 512)
+        sigmoid(2, 0, 0, 256)
+        sigmoid(2, 1, 0, 256)
+        first_product(2, [2, 3], 256, 512)
+        first_product(3, [0, 1], 0, 256)
+        first_product(3, [2, 3], 0, 256)
+        second_product(0, 0, 512, 0)
+        sigmoid(2, 2, 0, 256)
+        sigmoid(2, 3, 0, 256)
         round_w2("S", 1)
-        quant_h(1, 1)
-        scale_h(2, 0)
-        finish(0)
+        for t in range(4):
+            sigmoid(2, t, 256, 512)
+        sigmoid(3, 0, 0, 256)
+        sigmoid(3, 1, 0, 256)
+        scale_h(2, 0, 256)
         quant_w2(1)
-        sigmoid(3, 0)
-        first_product(3, 3)
-        second_product(1)
+        second_product(1, 0, 512, 1)
+        first_product(3, [0, 1], 256, 512)
+        quant_h(2, 0, 256)
+        finish(0, 0, 512, 0)
+        scale_h(2, 256, 512)
+        sigmoid(3, 2, 0, 256)
+        sigmoid(3, 3, 0, 256)
+        first_product(3, [2, 3], 256, 512)
         round_w2("S", 2)
-        scale_h(2, 1)
-        quant_h(2, 0)
-        finish(1)
-        sigmoid(3, 1)
-        sigmoid(3, 2)
-        sigmoid(3, 3, 0)
-        sigmoid(3, 3, 1)
-        sigmoid(3, 3, 2)
-        sigmoid(3, 3, 3)
+        for t in range(4):
+            sigmoid(3, t, 256, 512)
+        scale_h_on_scalar(3, 384, 512)
         round_w2("S", 3)
-        scale_h_on_scalar(3, 3)
-        scale_h_on_scalar(3, 2)
-        weave_h("S", 3, 3)
-        weave_h("S", 3, 2)
-        quant_h(2, 1)
+        weave_h("S", 3, 384, 512)
+        finish(1, 0, 512, 1)
         quant_w2(2)
-        second_product(2)
-        scale_h(3, 0)
-        scale_h(3, 1)
-        quant_h(3, 0)
+        quant_h(2, 256, 512)
+        second_product(2, 0, 512, 0)
+        scale_h(3, 0, 256)
+        scale_h(3, 256, 384)
+        quant_h(3, 0, 256)
         quant_w2(3)
-        quant_h(3, 1)
-        quant_h(3, 3)
-        quant_h(3, 2)
-        second_product(3)
-        finish(2)
-        finish(3, 0, 256)
-        finish(3, 256, 512)
+        second_product(3, 0, 256, 1)
+        quant_h(3, 256, 512)
+        second_product(3, 256, 512, 2)
+        finish(2, 0, 256, 0)
+        finish(2, 256, 512, 0)
+        finish(3, 0, 256, 1)
+        finish(3, 256, 512, 2)

@@ -23,7 +23,7 @@ RUN = 2
 NMM = 128
 Z_BANKS = (3, 2)
 X_PIECES = [[(0, 128), (128, 256), (256, 512)], [(0, 512)]]
-W1_PIECES = [[(0, 2), (2, 4)], [(0, 4)]]
+W1_PIECES = [[(0, 256), (256, 512)], [(0, 512)]]
 SIG_TILES = [[(0, 128, 128), (128, 256, 128), (256, 512, 256)]] * 2 + [[(0, 256, 256), (256, 512, 256)], [(0, 256, 256), (256, 512, 128)]]
 
 
@@ -37,7 +37,7 @@ def tile_rows_gmlp_sigmoid_bias_res_kernel(tc, x, w1, hs, w2, b, r, out):
         def tile(name, shape, dtype):
             return sb.tile(shape, dtype, name=name, align_bytes=64)
 
-        w1_raw = {(s, lo): tile("w1_raw%d_%d" % (s, lo), [P, hi - lo, K], F32) for s in range(PAIRS) for lo, hi in W1_PIECES[s]}
+        w1_raw = {(s, lo): tile("w1_raw%d_%d" % (s, lo), [P, PACK, hi - lo], F32) for s in range(PAIRS) for lo, hi in W1_PIECES[s]}
         w1_bf = [[tile("w1_bf%d%d" % (s, u), [P, 2 * PACK * P], BF16) for u in range(2)] for s in range(PAIRS)]
         w1_codes = [[tile("w1_codes%d%d" % (s, t), [P, P], U32) for t in range(PACK)] for s in range(PAIRS)]
         w1_scales = [[tile("w1_scales%d%d" % (s, t), [P, P], U8) for t in range(PACK)] for s in range(PAIRS)]
@@ -72,7 +72,7 @@ def tile_rows_gmlp_sigmoid_bias_res_kernel(tc, x, w1, hs, w2, b, r, out):
 
         def load_w1(s, i):
             lo, hi = W1_PIECES[s][i]
-            nc.sync.dma_start(out=w1_raw[s, lo][:], in_=pair(w1, s)[:, lo:hi, :])
+            nc.sync.dma_start(out=w1_raw[s, lo][:], in_=pair(w1, s)[:, :, lo:hi])
 
         def load_x(s, i):
             lo, hi = X_PIECES[s][i]
@@ -112,12 +112,13 @@ def tile_rows_gmlp_sigmoid_bias_res_kernel(tc, x, w1, hs, w2, b, r, out):
             else:
                 nc.scalar.copy(out=dst, in_=src)
 
-        def round_w1(engine, s, u, i=0, a=0, z=P):
-            lo, hi = W1_PIECES[s][i]
+        def round_w1(engine, s, u, a=0, z=P):
+            start = max(lo for lo, hi in W1_PIECES[s] if lo <= PACK * a)
+            first = start // PACK
             copy(
                 engine,
-                w1_bf[s][u][:].rearrange("p (e m j) -> p m j e", e=2, j=PACK)[:, a:z, lo:hi],
-                w1_raw[s, lo][:].rearrange("p j (m u e) -> p u m j e", u=2, e=2)[:, u, a:z],
+                w1_bf[s][u][:].rearrange("p (e m j) -> p m j e", e=2, j=PACK)[:, a:z],
+                w1_raw[s, start][:].rearrange("p j (m u e) -> p u m j e", u=2, e=2)[:, u, a - first : z - first],
             )
 
         def quant_w1(s, t):
@@ -239,10 +240,10 @@ def tile_rows_gmlp_sigmoid_bias_res_kernel(tc, x, w1, hs, w2, b, r, out):
             nc.sync.dma_start(out=out[g][:, lo:hi], in_=y_sb[g][:, lo:hi])
 
         clear_vectors()
-        load_x(0, 0)
-        load_vectors()
         load_w1(0, 0)
+        load_vectors()
         load_w1(0, 1)
+        load_x(0, 0)
         load_x(0, 1)
         load_x(0, 2)
         load_w1(1, 0)
@@ -253,23 +254,25 @@ def tile_rows_gmlp_sigmoid_bias_res_kernel(tc, x, w1, hs, w2, b, r, out):
         load_w2(1)
         load_r(2)
         load_r(3)
-        round_x("V", 0, 0, 128)
+        round_w1("V", 0, 0, 0, 64)
+        round_w1("V", 0, 1, 0, 64)
         deal_vectors()
-        quant_x(0, 0, 128)
         turn_vectors()
-        round_w1("V", 0, 0, 0)
-        gather_gain()
-        round_w1("V", 0, 1, 0)
-        round_w1("V", 0, 0, 1)
-        round_w1("V", 0, 1, 1)
-        for t in range(4):
-            quant_w1(0, t)
+        round_w1("V", 0, 0, 64, 128)
+        round_w1("V", 0, 1, 64, 128)
+        round_x("V", 0, 0, 128)
+        quant_w1(0, 0)
+        quant_w1(0, 1)
+        quant_x(0, 0, 128)
+        quant_w1(0, 2)
+        quant_w1(0, 3)
         first_product(0, [0], 0, 128)
         first_product(0, [1], 0, 128)
         first_product(0, [2, 3], 0, 128)
         first_product(1, [0, 1], 0, 128)
         first_product(1, [2, 3], 0, 128)
         round_x("V", 0, 128, 256)
+        gather_gain()
         for t in range(4):
             sigmoid(0, t, 0, 128)
         quant_x(0, 128, 256)
@@ -293,14 +296,14 @@ def tile_rows_gmlp_sigmoid_bias_res_kernel(tc, x, w1, hs, w2, b, r, out):
         for t in range(4):
             sigmoid(0, t, 256, 512)
         round_w1("S", 1, 1)
-        round_x("S", 1, 256, 512)
+        round_x("S", 1, 288, 512)
         for t in range(4):
             sigmoid(1, t, 256, 512)
         round_w1("V", 1, 0)
         scale_h(1, 128, 256)
         quant_h(0, 0, 256)
         quant_h(1, 0, 256)
-        round_x("V", 1, 0, 256)
+        round_x("V", 1, 0, 288)
         for t in range(4):
             quant_w1(1, t)
         quant_x(1, 0, 256)

@@ -23,8 +23,8 @@ RUN = 2
 NMM = 128
 Z_BANKS = (3, 2)
 X_PIECES = [[(0, 128), (128, 256), (256, 512)], [(0, 512)]]
-W1_PIECES = [[(0, 256), (256, 512)], [(0, 512)]]
-SIG_TILES = [[(0, 128, 128), (128, 256, 128), (256, 512, 256)]] * 2 + [[(0, 256, 256), (256, 512, 256)], [(0, 256, 256), (256, 512, 128)]]
+W1_PIECES = [[(0, 512)], [(0, 512)]]
+SIG_TILES = [[(0, 128, 128), (128, 256, 128), (256, 512, 128)], [(0, 128, 128), (128, 256, 128), (256, 512, 256)], [(0, 256, 256), (256, 512, 256)], [(0, 256, 256), (256, 512, 128)]]
 
 
 def tile_rows_gmlp_sigmoid_bias_res_kernel(tc, x, w1, hs, w2, b, r, out):
@@ -53,6 +53,7 @@ def tile_rows_gmlp_sigmoid_bias_res_kernel(tc, x, w1, hs, w2, b, r, out):
         vec_rows = tile("vec_rows", [P, P], F32)
         vec_dealt = tile("vec_dealt", [P, P], F32)
         vec_turned = tile("vec_turned", [P, P], F32)
+        warm = tile("warm", [P, 2], F32)
         gain = tile("gain", [P, G, PACK], F32)
 
         sig = {(g, lo): tile("sig%d_%d" % (g, lo), [P, (hi - lo) // w, PACK, w], F32) for g in range(G) for lo, hi, w in SIG_TILES[g]}
@@ -90,6 +91,10 @@ def tile_rows_gmlp_sigmoid_bias_res_kernel(tc, x, w1, hs, w2, b, r, out):
         def load_vectors():
             for v, src in enumerate((b, hs)):
                 nc.sync.dma_start(out=vec_rows[4 * v : P : 8, :], in_=src.rearrange("g (q a) o -> q g (a o)", q=4))
+
+        def warm_table():
+            nc.vector.memset(warm[:, 0:1], 0.0)
+            nc.scalar.activation(out=warm[:, 1:2], in_=warm[:, 0:1], func=SIGMOID)
 
         def clear_vectors():
             nc.vector.memset(vec_rows[:], 0.0)
@@ -240,124 +245,128 @@ def tile_rows_gmlp_sigmoid_bias_res_kernel(tc, x, w1, hs, w2, b, r, out):
             nc.sync.dma_start(out=out[g][:, lo:hi], in_=y_sb[g][:, lo:hi])
 
         clear_vectors()
+        warm_table()
         load_w1(0, 0)
         load_vectors()
-        load_w1(0, 1)
         load_x(0, 0)
         load_x(0, 1)
         load_x(0, 2)
         load_w1(1, 0)
         load_x(1, 0)
         load_w2(0)
-        load_r(0)
-        load_r(1)
         load_w2(1)
-        load_r(2)
-        load_r(3)
-        round_w1("V", 0, 0, 0, 64)
-        round_w1("V", 0, 1, 0, 64)
+        for g in range(G):
+            load_r(g)
         deal_vectors()
+        round_w1("V", 0, 0)
+        round_w1("S", 0, 1)
         turn_vectors()
-        round_w1("V", 0, 0, 64, 128)
-        round_w1("V", 0, 1, 64, 128)
         round_x("V", 0, 0, 128)
         quant_w1(0, 0)
-        quant_w1(0, 1)
         quant_x(0, 0, 128)
+        first_product(0, [0], 0, 128)
+        quant_w1(0, 1)
+        first_product(0, [1], 0, 128)
         quant_w1(0, 2)
         quant_w1(0, 3)
-        first_product(0, [0], 0, 128)
-        first_product(0, [1], 0, 128)
         first_product(0, [2, 3], 0, 128)
         first_product(1, [0, 1], 0, 128)
         first_product(1, [2, 3], 0, 128)
         round_x("V", 0, 128, 256)
         gather_gain()
+        quant_x(0, 128, 256)
         for t in range(4):
             sigmoid(0, t, 0, 128)
-        quant_x(0, 128, 256)
-        first_product(0, [0, 1, 2, 3], 128, 256)
+        first_product(0, [0, 1], 128, 256)
+        first_product(0, [2, 3], 128, 256)
         for t in range(4):
             sigmoid(1, t, 0, 128)
-        first_product(1, [0, 1, 2, 3], 128, 256)
+        first_product(1, [0, 1], 128, 256)
+        first_product(1, [2, 3], 128, 256)
         round_x("V", 0, 256, 512)
         scale_h(0, 0, 128)
         quant_x(0, 256, 512)
         first_product(0, [0, 1], 256, 512)
-        first_product(0, [2, 3], 256, 512)
-        first_product(1, [0, 1], 256, 512)
         for t in range(4):
             sigmoid(0, t, 128, 256)
+        first_product(0, [2, 3], 256, 512)
         for t in range(4):
             sigmoid(1, t, 128, 256)
+        first_product(1, [0, 1], 256, 512)
         first_product(1, [2, 3], 256, 512)
         scale_h(1, 0, 128)
+        round_w1("S", 1, 1, 0, 64)
         scale_h(0, 128, 256)
+        round_w1("V", 1, 0)
+        round_w1("V", 1, 1, 64, 128)
         for t in range(4):
             sigmoid(0, t, 256, 512)
-        round_w1("S", 1, 1)
-        round_x("S", 1, 288, 512)
-        for t in range(4):
-            sigmoid(1, t, 256, 512)
-        round_w1("V", 1, 0)
+        sigmoid(1, 0, 256, 512)
+        sigmoid(1, 1, 256, 512)
+        scale_h_on_scalar(0, 384, 512)
+        sigmoid(1, 2, 256, 512)
+        sigmoid(1, 3, 256, 512)
+        weave_h("S", 0, 384, 512)
         scale_h(1, 128, 256)
-        quant_h(0, 0, 256)
-        quant_h(1, 0, 256)
-        round_x("V", 1, 0, 288)
-        for t in range(4):
-            quant_w1(1, t)
+        quant_w1(1, 0)
+        quant_w1(1, 1)
+        round_x("V", 1, 0, 256)
+        quant_w1(1, 2)
+        quant_w1(1, 3)
         quant_x(1, 0, 256)
         first_product(2, [0, 1], 0, 256)
         first_product(2, [2, 3], 0, 256)
-        round_w2("S", 0)
-        scale_h(0, 256, 512)
-        quant_x(1, 256, 512)
-        first_product(2, [0, 1], 256, 512)
-        scale_h(1, 256, 512)
-        quant_h(0, 256, 512)
-        quant_w2(0)
-        quant_h(1, 256, 512)
-        sigmoid(2, 0, 0, 256)
-        sigmoid(2, 1, 0, 256)
-        first_product(2, [2, 3], 256, 512)
         first_product(3, [0, 1], 0, 256)
         first_product(3, [2, 3], 0, 256)
+        round_x("S", 1, 384, 512)
+        round_x("V", 1, 256, 384)
+        quant_h(0, 0, 256)
+        scale_h(0, 256, 384)
+        quant_h(1, 0, 256)
+        quant_h(0, 256, 512)
+        quant_x(1, 256, 512)
+        first_product(2, [0, 1], 256, 512)
+        for t in range(4):
+            sigmoid(2, t, 0, 256)
+        first_product(2, [2, 3], 256, 512)
+        round_w2("S", 0, 2)
+        scale_h(1, 256, 512)
+        scale_h(2, 0, 256)
+        quant_w2(0, 2)
         second_product(0, 0, 512, 0)
-        sigmoid(2, 2, 0, 256)
-        sigmoid(2, 3, 0, 256)
-        round_w2("S", 1)
+        quant_h(1, 256, 512)
         for t in range(4):
             sigmoid(2, t, 256, 512)
+        quant_h(2, 0, 256)
+        scale_h(2, 256, 512)
+        finish(0, 0, 512, 0)
         sigmoid(3, 0, 0, 256)
         sigmoid(3, 1, 0, 256)
-        scale_h(2, 0, 256)
-        quant_w2(1)
-        second_product(1, 0, 512, 1)
         first_product(3, [0, 1], 256, 512)
-        quant_h(2, 0, 256)
-        finish(0, 0, 512, 0)
-        scale_h(2, 256, 512)
         sigmoid(3, 2, 0, 256)
         sigmoid(3, 3, 0, 256)
         first_product(3, [2, 3], 256, 512)
+        second_product(1, 0, 512, 1)
         round_w2("S", 2)
+        scale_h(3, 0, 256)
+        quant_h(2, 256, 512)
+        quant_w2(2)
+        second_product(2, 0, 512, 0)
+        finish(1, 0, 512, 1)
         for t in range(4):
             sigmoid(3, t, 256, 512)
         scale_h_on_scalar(3, 384, 512)
         round_w2("S", 3)
         weave_h("S", 3, 384, 512)
-        finish(1, 0, 512, 1)
-        quant_w2(2)
-        quant_h(2, 256, 512)
-        second_product(2, 0, 512, 0)
-        scale_h(3, 0, 256)
         scale_h(3, 256, 384)
         quant_h(3, 0, 256)
         quant_w2(3)
         second_product(3, 0, 256, 1)
-        quant_h(3, 256, 512)
-        second_product(3, 256, 512, 2)
+        quant_h(3, 256, 384)
+        second_product(3, 256, 384, 1)
         finish(2, 0, 256, 0)
+        quant_h(3, 384, 512)
+        second_product(3, 384, 512, 2)
         finish(2, 256, 512, 0)
-        finish(3, 0, 256, 1)
-        finish(3, 256, 512, 2)
+        finish(3, 0, 384, 1)
+        finish(3, 384, 512, 2)

@@ -257,11 +257,11 @@ def tile_rows_gmlp_sigmoid_bias_res_kernel(tc, x, w1, hs, w2, b, r, out):
         load_w2(1)
         for g in range(G):
             load_r(g)
-        deal_vectors()
         round_w1("V", 0, 0)
         round_w1("S", 0, 1)
-        turn_vectors()
+        deal_vectors()
         round_x("V", 0, 0, 128)
+        turn_vectors()
         quant_w1(0, 0)
         quant_x(0, 0, 128)
         first_product(0, [0], 0, 128)
@@ -316,29 +316,30 @@ def tile_rows_gmlp_sigmoid_bias_res_kernel(tc, x, w1, hs, w2, b, r, out):
         quant_x(1, 0, 256)
         first_product(2, [0, 1], 0, 256)
         first_product(2, [2, 3], 0, 256)
-        first_product(3, [0, 1], 0, 256)
-        first_product(3, [2, 3], 0, 256)
-        round_x("S", 1, 384, 512)
-        round_x("V", 1, 256, 384)
+        round_x("V", 1, 256, 512)
         quant_h(0, 0, 256)
-        scale_h(0, 256, 384)
-        quant_h(1, 0, 256)
-        quant_h(0, 256, 512)
         quant_x(1, 256, 512)
         first_product(2, [0, 1], 256, 512)
+        scale_h(0, 256, 384)
+        quant_h(1, 0, 256)
+        scale_h(1, 256, 512)
         for t in range(4):
             sigmoid(2, t, 0, 256)
         first_product(2, [2, 3], 256, 512)
-        round_w2("S", 0, 2)
-        scale_h(1, 256, 512)
+        first_product(3, [0, 1], 0, 256)
+        first_product(3, [2, 3], 0, 256)
+        round_w2("S", 0)
+        quant_h(0, 256, 512)
         scale_h(2, 0, 256)
-        quant_w2(0, 2)
+        quant_w2(0)
         second_product(0, 0, 512, 0)
         quant_h(1, 256, 512)
         for t in range(4):
             sigmoid(2, t, 256, 512)
+        round_w2("S", 1)
         quant_h(2, 0, 256)
         scale_h(2, 256, 512)
+        quant_w2(1)
         finish(0, 0, 512, 0)
         sigmoid(3, 0, 0, 256)
         sigmoid(3, 1, 0, 256)
@@ -348,8 +349,8 @@ def tile_rows_gmlp_sigmoid_bias_res_kernel(tc, x, w1, hs, w2, b, r, out):
         first_product(3, [2, 3], 256, 512)
         second_product(1, 0, 512, 1)
         round_w2("S", 2)
-        scale_h(3, 0, 256)
         quant_h(2, 256, 512)
+        scale_h(3, 0, 256)
         quant_w2(2)
         second_product(2, 0, 512, 0)
         finish(1, 0, 512, 1)
@@ -362,11 +363,9 @@ def tile_rows_gmlp_sigmoid_bias_res_kernel(tc, x, w1, hs, w2, b, r, out):
         quant_h(3, 0, 256)
         quant_w2(3)
         second_product(3, 0, 256, 1)
-        quant_h(3, 256, 384)
-        second_product(3, 256, 384, 1)
+        quant_h(3, 256, 512)
+        second_product(3, 256, 512, 2)
         finish(2, 0, 256, 0)
-        quant_h(3, 384, 512)
-        second_product(3, 384, 512, 2)
         finish(2, 256, 512, 0)
-        finish(3, 0, 384, 1)
-        finish(3, 384, 512, 2)
+        finish(3, 0, 256, 1)
+        finish(3, 256, 512, 2)

@@ -38,9 +38,9 @@ def tile_rows_gmlp_sigmoid_bias_res_kernel(tc, x, w1, hs, w2, b, r, out):
             return sb.tile(shape, dtype, name=name, align_bytes=64)
 
         w1_raw = {(s, lo): tile("w1_raw%d_%d" % (s, lo), [P, PACK, hi - lo], F32) for s in range(PAIRS) for lo, hi in W1_PIECES[s]}
-        w1_bf = [[tile("w1_bf%d%d" % (s, u), [P, 2 * PACK * P], BF16) for u in range(2)] for s in range(PAIRS)]
-        w1_codes = [[tile("w1_codes%d%d" % (s, t), [P, P], U32) for t in range(PACK)] for s in range(PAIRS)]
-        w1_scales = [[tile("w1_scales%d%d" % (s, t), [P, P], U8) for t in range(PACK)] for s in range(PAIRS)]
+        w1_bf = [tile("w1_bf%d" % s, [P, PACK * K], BF16) for s in range(PAIRS)]
+        w1_codes = [tile("w1_codes%d" % s, [P, K], U32) for s in range(PAIRS)]
+        w1_scales = [tile("w1_scales%d" % s, [P, K], U8) for s in range(PAIRS)]
         x_raw = {(s, lo): tile("x_raw%d_%d" % (s, lo), [P, PACK, hi - lo], F32) for s in range(PAIRS) for lo, hi in X_PIECES[s]}
         x_bf = [tile("x_bf%d" % s, [P, PACK * N], BF16) for s in range(PAIRS)]
         x_codes = [tile("x_codes%d" % s, [P, N], U32) for s in range(PAIRS)]
@@ -122,16 +122,15 @@ def tile_rows_gmlp_sigmoid_bias_res_kernel(tc, x, w1, hs, w2, b, r, out):
             first = start // PACK
             copy(
                 engine,
-                w1_bf[s][u][:].rearrange("p (e m j) -> p m j e", e=2, j=PACK)[:, a:z],
+                w1_bf[s][:, 2 * u * PACK * P : 2 * (u + 1) * PACK * P].rearrange("p (e m j) -> p m j e", e=2, j=PACK)[:, a:z],
                 w1_raw[s, start][:].rearrange("p j (m u e) -> p u m j e", u=2, e=2)[:, u, a - first : z - first],
             )
 
-        def quant_w1(s, t):
-            u, e = divmod(t, 2)
+        def quant_w1(s, t, count=1):
             nc.vector.quantize_mx(
-                out=w1_codes[s][t][:].bitcast(FP8X4),
-                scales=w1_scales[s][t][:],
-                in_=w1_bf[s][u][:, e * PACK * P : (e + 1) * PACK * P],
+                out=w1_codes[s][:, t * P : (t + count) * P].bitcast(FP8X4),
+                scales=w1_scales[s][:, t * P : (t + count) * P],
+                in_=w1_bf[s][:, t * PACK * P : (t + count) * PACK * P],
             )
 
         def round_x(engine, s, lo, hi):
@@ -174,8 +173,8 @@ def tile_rows_gmlp_sigmoid_bias_res_kernel(tc, x, w1, hs, w2, b, r, out):
                     z_place[g, t, col] = (bank, base)
                     nc.tensor.matmul_mx(
                         out=bank[:, base + col : base + col + NMM],
-                        lhsT=w1_codes[s][t][rows, :].bitcast(FP8X4),
-                        lhsT_scale=w1_scales[s][t][rows, :],
+                        lhsT=w1_codes[s][rows, t * P : (t + 1) * P].bitcast(FP8X4),
+                        lhsT_scale=w1_scales[s][rows, t * P : (t + 1) * P],
                         rhs=x_codes[s][rows, col : col + NMM].bitcast(FP8X4),
                         rhs_scale=x_scales[s][rows, col : col + NMM],
                         start=True,
@@ -264,28 +263,31 @@ def tile_rows_gmlp_sigmoid_bias_res_kernel(tc, x, w1, hs, w2, b, r, out):
         turn_vectors()
         quant_w1(0, 0)
         quant_x(0, 0, 128)
+        round_x("S", 0, 128, 256)
         first_product(0, [0], 0, 128)
         quant_w1(0, 1)
         first_product(0, [1], 0, 128)
-        quant_w1(0, 2)
-        quant_w1(0, 3)
-        first_product(0, [2, 3], 0, 128)
         first_product(1, [0, 1], 0, 128)
+        quant_w1(0, 2, 2)
+        first_product(0, [2, 3], 0, 128)
         first_product(1, [2, 3], 0, 128)
-        round_x("V", 0, 128, 256)
         gather_gain()
         quant_x(0, 128, 256)
-        for t in range(4):
-            sigmoid(0, t, 0, 128)
+        for g in range(2):
+            sigmoid(g, 0, 0, 128)
+            sigmoid(g, 1, 0, 128)
         first_product(0, [0, 1], 128, 256)
         first_product(0, [2, 3], 128, 256)
-        for t in range(4):
-            sigmoid(1, t, 0, 128)
         first_product(1, [0, 1], 128, 256)
+        for g in range(2):
+            sigmoid(g, 2, 0, 128)
+            sigmoid(g, 3, 0, 128)
         first_product(1, [2, 3], 128, 256)
-        round_x("V", 0, 256, 512)
+        round_x("V", 0, 256, 384)
+        round_x("V", 0, 384, 512)
+        quant_x(0, 256, 384)
         scale_h(0, 0, 128)
-        quant_x(0, 256, 512)
+        quant_x(0, 384, 512)
         first_product(0, [0, 1], 256, 512)
         for t in range(4):
             sigmoid(0, t, 128, 256)
@@ -297,47 +299,44 @@ def tile_rows_gmlp_sigmoid_bias_res_kernel(tc, x, w1, hs, w2, b, r, out):
         scale_h(1, 0, 128)
         round_w1("S", 1, 1, 0, 64)
         scale_h(0, 128, 256)
-        round_w1("V", 1, 0)
         round_w1("V", 1, 1, 64, 128)
+        round_w1("V", 1, 0)
         for t in range(4):
             sigmoid(0, t, 256, 512)
         sigmoid(1, 0, 256, 512)
         sigmoid(1, 1, 256, 512)
         scale_h_on_scalar(0, 384, 512)
+        round_x("S", 1, 384, 512)
         sigmoid(1, 2, 256, 512)
         sigmoid(1, 3, 256, 512)
         weave_h("S", 0, 384, 512)
-        scale_h(1, 128, 256)
-        quant_w1(1, 0)
-        quant_w1(1, 1)
+        quant_w1(1, 2, 2)
+        quant_w1(1, 0, 2)
+        quant_h(0, 0, 256)
         round_x("V", 1, 0, 256)
-        quant_w1(1, 2)
-        quant_w1(1, 3)
+        round_x("V", 1, 256, 384)
         quant_x(1, 0, 256)
         first_product(2, [0, 1], 0, 256)
         first_product(2, [2, 3], 0, 256)
-        round_x("V", 1, 256, 512)
-        quant_h(0, 0, 256)
+        scale_h(1, 128, 256)
         quant_x(1, 256, 512)
         first_product(2, [0, 1], 256, 512)
-        scale_h(0, 256, 384)
-        quant_h(1, 0, 256)
-        scale_h(1, 256, 512)
         for t in range(4):
             sigmoid(2, t, 0, 256)
         first_product(2, [2, 3], 256, 512)
         first_product(3, [0, 1], 0, 256)
         first_product(3, [2, 3], 0, 256)
         round_w2("S", 0)
+        scale_h(0, 256, 384)
+        scale_h(1, 256, 512)
         quant_h(0, 256, 512)
         scale_h(2, 0, 256)
         quant_w2(0)
         second_product(0, 0, 512, 0)
-        quant_h(1, 256, 512)
+        quant_h(1, 0, 512)
         for t in range(4):
             sigmoid(2, t, 256, 512)
         round_w2("S", 1)
-        quant_h(2, 0, 256)
         scale_h(2, 256, 512)
         quant_w2(1)
         finish(0, 0, 512, 0)
@@ -349,7 +348,7 @@ def tile_rows_gmlp_sigmoid_bias_res_kernel(tc, x, w1, hs, w2, b, r, out):
         first_product(3, [2, 3], 256, 512)
         second_product(1, 0, 512, 1)
         round_w2("S", 2)
-        quant_h(2, 256, 512)
+        quant_h(2, 0, 512)
         scale_h(3, 0, 256)
         quant_w2(2)
         second_product(2, 0, 512, 0)

@@ -21,10 +21,18 @@ ROWS = 64
 PAIRS = 2
 RUN = 2
 NMM = 128
+WORDS = {"w1": 2 * P, "x": N, "w2": M, "h": N}
 Z_BANKS = (3, 2)
-X_PIECES = [[(0, 128), (128, 256), (256, 512)], [(0, 512)]]
-W1_PIECES = [[(0, 512)], [(0, 512)]]
-SIG_TILES = [[(0, 128, 128), (128, 256, 128), (256, 512, 128)], [(0, 128, 128), (128, 256, 128), (256, 512, 256)], [(0, 256, 256), (256, 512, 256)], [(0, 256, 256), (256, 512, 128)]]
+X_PIECES = [[(0, 128, 0, 4), (128, 256, 0, 4), (256, 512, 0, 2), (256, 512, 2, 4)], [(0, 512, 0, 4)]]
+STRIPS = [
+    [("w1", 0, 0), ("w1", 0, 1)],
+    [("x", 0)],
+    [("x", 1)],
+    [("w1", 1, 1), ("w1", 1, 0), ("h", 0)],
+    [("h", 1), ("w2", 0)],
+    [("w2", 1), ("h", 2), ("w2", 2)],
+    [("w2", 3), ("h", 3)],
+]
 
 
 def tile_rows_gmlp_sigmoid_bias_res_kernel(tc, x, w1, hs, w2, b, r, out):
@@ -37,18 +45,35 @@ def tile_rows_gmlp_sigmoid_bias_res_kernel(tc, x, w1, hs, w2, b, r, out):
         def tile(name, shape, dtype):
             return sb.tile(shape, dtype, name=name, align_bytes=64)
 
-        w1_raw = {(s, lo): tile("w1_raw%d_%d" % (s, lo), [P, PACK, hi - lo], F32) for s in range(PAIRS) for lo, hi in W1_PIECES[s]}
-        w1_bf = [tile("w1_bf%d" % s, [P, PACK * K], BF16) for s in range(PAIRS)]
-        w1_codes = [tile("w1_codes%d" % s, [P, K], U32) for s in range(PAIRS)]
-        w1_scales = [tile("w1_scales%d" % s, [P, K], U8) for s in range(PAIRS)]
-        x_raw = {(s, lo): tile("x_raw%d_%d" % (s, lo), [P, PACK, hi - lo], F32) for s in range(PAIRS) for lo, hi in X_PIECES[s]}
-        x_bf = [tile("x_bf%d" % s, [P, PACK * N], BF16) for s in range(PAIRS)]
-        x_codes = [tile("x_codes%d" % s, [P, N], U32) for s in range(PAIRS)]
-        x_scales = [tile("x_scales%d" % s, [P, N], U8) for s in range(PAIRS)]
+        place = {}
+        for i, names in enumerate(STRIPS):
+            words = sum(WORDS[name[0]] for name in names)
+            strip = (tile("rounded%d" % i, [P, PACK * words], BF16), tile("codes%d" % i, [P, words], U32), tile("scales%d" % i, [P, words], U8))
+            start = 0
+            for name in names:
+                place[name] = (strip, start)
+                start = start + WORDS[name[0]]
+
+        def rounded(name, lo, hi):
+            strip, start = place[name]
+            return strip[0][:, PACK * (start + lo) : PACK * (start + hi)]
+
+        def codes(name, lo, hi, rows=slice(0, P)):
+            strip, start = place[name]
+            return strip[1][rows, start + lo : start + hi].bitcast(FP8X4)
+
+        def scales(name, lo, hi, rows=slice(0, P)):
+            strip, start = place[name]
+            return strip[2][rows, start + lo : start + hi]
+
+        def quant(name, lo, hi):
+            nc.vector.quantize_mx(out=codes(name, lo, hi), scales=scales(name, lo, hi), in_=rounded(name, lo, hi))
+
+        w1_raw = [tile("w1_raw%d" % s, [P, PACK, K], F32) for s in range(PAIRS)]
+        x_raw = {
+            (s, lo, j0): tile("x_raw%d_%d_%d" % (s, lo, j0), [P, j1 - j0, hi - lo], F32) for s in range(PAIRS) for lo, hi, j0, j1 in X_PIECES[s]
+        }
         w2_raw = [tile("w2_raw%d" % s, [P, 2, PACK, M], F32) for s in range(PAIRS)]
-        w2_bf = [tile("w2_bf%d" % s, [P, 2 * PACK * M], BF16) for s in range(PAIRS)]
-        w2_codes = [tile("w2_codes%d" % s, [P, 2 * M], U32) for s in range(PAIRS)]
-        w2_scales = [tile("w2_scales%d" % s, [P, 2 * M], U8) for s in range(PAIRS)]
         r_sb = [tile("r_sb%d" % g, [P, N], F32) for g in range(G)]
         vec_rows = tile("vec_rows", [P, P], F32)
         vec_dealt = tile("vec_dealt", [P, P], F32)
@@ -56,28 +81,24 @@ def tile_rows_gmlp_sigmoid_bias_res_kernel(tc, x, w1, hs, w2, b, r, out):
         warm = tile("warm", [P, 2], F32)
         gain = tile("gain", [P, G, PACK], F32)
 
-        sig = {(g, lo): tile("sig%d_%d" % (g, lo), [P, (hi - lo) // w, PACK, w], F32) for g in range(G) for lo, hi, w in SIG_TILES[g]}
+        sig = {}
         h_rows = {}
-        h_bf = [tile("h_bf%d" % g, [P, PACK * N], BF16) for g in range(G)]
-        h_codes = [tile("h_codes%d" % g, [P, N], U32) for g in range(G)]
-        h_scales = [tile("h_scales%d" % g, [P, N], U8) for g in range(G)]
         y_sb = [tile("y_sb%d" % g, [P, N], F32) for g in range(G)]
 
         z_banks = [[ps.tile([P, N], F32, name="z%d%d" % (c, i)) for i in range(Z_BANKS[c])] for c in range(2)]
-        y_banks = [ps.tile([P, N], F32, name="y%d" % i) for i in range(3)]
+        y_banks = [ps.tile([P, N], F32, name="y%d" % i) for i in range(8 - sum(Z_BANKS))]
         z_turn = [0, 0]
         z_place = {}
 
         def pair(t, s):
             return t[2 * s : 2 * s + 2].rearrange("g (p j) n -> (g p) j n", j=PACK)
 
-        def load_w1(s, i):
-            lo, hi = W1_PIECES[s][i]
-            nc.sync.dma_start(out=w1_raw[s, lo][:], in_=pair(w1, s)[:, :, lo:hi])
+        def load_w1(s):
+            nc.sync.dma_start(out=w1_raw[s][:], in_=pair(w1, s))
 
         def load_x(s, i):
-            lo, hi = X_PIECES[s][i]
-            nc.sync.dma_start(out=x_raw[s, lo][:], in_=pair(x, s)[:, :, lo:hi])
+            lo, hi, j0, j1 = X_PIECES[s][i]
+            nc.sync.dma_start(out=x_raw[s, lo, j0][:], in_=pair(x, s)[:, j0:j1, lo:hi])
 
         def load_w2(s):
             nc.sync.dma_start(
@@ -99,67 +120,42 @@ def tile_rows_gmlp_sigmoid_bias_res_kernel(tc, x, w1, hs, w2, b, r, out):
         def clear_vectors():
             nc.vector.memset(vec_rows[:], 0.0)
 
-        def deal_vectors():
-            nc.vector.tensor_copy(
-                out=vec_dealt[:].rearrange("p (t s) -> p t s", t=PACK),
-                in_=vec_rows[:].rearrange("p (s t) -> p t s", t=PACK),
-            )
-
-        def turn_vectors():
-            nc.vector.transpose(out=vec_turned[:], in_=vec_dealt[:])
-
-        def gather_gain():
-            nc.vector.tensor_copy(out=gain[:], in_=vec_turned[:].rearrange("p (t g z) -> p g t z", t=PACK, g=G)[:, :, :, 4])
-
         def copy(engine, dst, src):
             if engine == "V":
                 nc.vector.tensor_copy(out=dst, in_=src)
             else:
                 nc.scalar.copy(out=dst, in_=src)
 
+        def deal_vectors(engine):
+            copy(engine, vec_dealt[:].rearrange("p (t s) -> p t s", t=PACK), vec_rows[:].rearrange("p (s t) -> p t s", t=PACK))
+
+        def turn_vectors():
+            nc.vector.transpose(out=vec_turned[:], in_=vec_dealt[:])
+
+        def gather_gain(engine):
+            copy(engine, gain[:], vec_turned[:].rearrange("p (t g z) -> p g t z", t=PACK, g=G)[:, :, :, 4])
+
         def round_w1(engine, s, u, a=0, z=P):
-            start = max(lo for lo, hi in W1_PIECES[s] if lo <= PACK * a)
-            first = start // PACK
             copy(
                 engine,
-                w1_bf[s][:, 2 * u * PACK * P : 2 * (u + 1) * PACK * P].rearrange("p (e m j) -> p m j e", e=2, j=PACK)[:, a:z],
-                w1_raw[s, start][:].rearrange("p j (m u e) -> p u m j e", u=2, e=2)[:, u, a - first : z - first],
+                rounded(("w1", s, u), 0, 2 * P).rearrange("p (e m j) -> p m j e", e=2, j=PACK)[:, a:z],
+                w1_raw[s][:].rearrange("p j (m u e) -> p u m j e", u=2, e=2)[:, u, a:z],
             )
 
-        def quant_w1(s, t, count=1):
-            nc.vector.quantize_mx(
-                out=w1_codes[s][:, t * P : (t + count) * P].bitcast(FP8X4),
-                scales=w1_scales[s][:, t * P : (t + count) * P],
-                in_=w1_bf[s][:, t * PACK * P : (t + count) * PACK * P],
-            )
-
-        def round_x(engine, s, lo, hi):
-            start = max(a for a, z in X_PIECES[s] if a <= lo)
+        def round_x(engine, s, lo, hi, j0=0, j1=PACK):
+            start = max(piece[0] for piece in X_PIECES[s] if piece[0] <= lo)
             copy(
                 engine,
-                x_bf[s][:, PACK * lo : PACK * hi].rearrange("p (c i j) -> p c j i", i=RUN, j=PACK),
-                x_raw[s, start][:, :, lo - start : hi - start].rearrange("p j (c i) -> p c j i", i=RUN),
+                rounded(("x", s), lo, hi).rearrange("p (c i j) -> p c j i", i=RUN, j=PACK)[:, :, j0:j1],
+                x_raw[s, start, j0][:, :, lo - start : hi - start].rearrange("p j (c i) -> p c j i", i=RUN),
             )
 
-        def quant_x(s, lo, hi):
-            nc.vector.quantize_mx(
-                out=x_codes[s][:, lo:hi].bitcast(FP8X4), scales=x_scales[s][:, lo:hi], in_=x_bf[s][:, PACK * lo : PACK * hi]
-            )
-
-        def round_w2(engine, g, count=1):
+        def round_w2(engine, g):
             s, c = divmod(g, 2)
             copy(
                 engine,
-                w2_bf[s][:, c * PACK * M : (c + count) * PACK * M].rearrange("p (g c i j) -> p g c j i", g=count, i=RUN, j=PACK),
-                w2_raw[s][:, c : c + count].rearrange("p g j (c i) -> p g c j i", i=RUN),
-            )
-
-        def quant_w2(g, count=1):
-            s, c = divmod(g, 2)
-            nc.vector.quantize_mx(
-                out=w2_codes[s][:, c * M : (c + count) * M].bitcast(FP8X4),
-                scales=w2_scales[s][:, c * M : (c + count) * M],
-                in_=w2_bf[s][:, c * PACK * M : (c + count) * PACK * M],
+                rounded(("w2", g), 0, M).rearrange("p (c i j) -> p c j i", i=RUN, j=PACK),
+                w2_raw[s][:, c].rearrange("p j (c i) -> p c j i", i=RUN),
             )
 
         def first_product(g, places, lo, hi):
@@ -169,72 +165,62 @@ def tile_rows_gmlp_sigmoid_bias_res_kernel(tc, x, w1, hs, w2, b, r, out):
             z_turn[c] = z_turn[c] + 1
             for n, t in enumerate(places):
                 base = n * (hi - lo) - lo
+                z_place[g, t, lo] = (bank, base)
                 for col in range(lo, hi, NMM):
-                    z_place[g, t, col] = (bank, base)
                     nc.tensor.matmul_mx(
                         out=bank[:, base + col : base + col + NMM],
-                        lhsT=w1_codes[s][rows, t * P : (t + 1) * P].bitcast(FP8X4),
-                        lhsT_scale=w1_scales[s][rows, t * P : (t + 1) * P],
-                        rhs=x_codes[s][rows, col : col + NMM].bitcast(FP8X4),
-                        rhs_scale=x_scales[s][rows, col : col + NMM],
+                        lhsT=codes(("w1", s, t // 2), t % 2 * P, (t % 2 + 1) * P, rows),
+                        lhsT_scale=scales(("w1", s, t // 2), t % 2 * P, (t % 2 + 1) * P, rows),
+                        rhs=codes(("x", s), col, col + NMM, rows),
+                        rhs_scale=scales(("x", s), col, col + NMM, rows),
                         start=True,
                         stop=True,
                     )
 
-        def sig_tile(g, lo):
-            return max((start, w) for start, end, w in SIG_TILES[g] if start <= lo)
+        def sigmoid(g, places, lo, hi):
+            if (g, lo) not in sig:
+                sig[g, lo] = tile("sig%d_%d" % (g, lo), [P, PACK, hi - lo], F32)
+            for t in places:
+                bank, base = z_place[g, t, lo]
+                nc.scalar.activation(
+                    out=sig[g, lo][:, t, :],
+                    in_=bank[:, base + lo : base + hi],
+                    func=SIGMOID,
+                    bias=vec_turned[:, 32 * t + 8 * g : 32 * t + 8 * g + 1],
+                )
 
         def sig_part(g, lo, hi):
-            start, w = sig_tile(g, lo)
-            assert hi - lo == w
-            return sig[g, start][:, (lo - start) // w]
-
-        def sigmoid(g, t, lo, hi):
-            bank, base = z_place[g, t, lo]
-            start, w = sig_tile(g, lo)
-            nc.scalar.activation(
-                out=sig[g, start][:, (lo - start) // w : (hi - start) // w, t, :],
-                in_=bank[:, base + lo : base + hi].rearrange("p (a w) -> p a w", w=w),
-                func=SIGMOID,
-                bias=vec_turned[:, 32 * t + 8 * g : 32 * t + 8 * g + 1],
-            )
+            start = max(a for q, a in sig if q == g and a <= lo)
+            return sig[g, start][:, :, lo - start : hi - start]
 
         def scale_h(g, lo, hi):
             nc.vector.tensor_tensor(
-                out=h_bf[g][:, PACK * lo : PACK * hi].rearrange("p (c i t) -> p c t i", i=RUN, t=PACK),
+                out=rounded(("h", g), lo, hi).rearrange("p (c i t) -> p c t i", i=RUN, t=PACK),
                 in0=sig_part(g, lo, hi).rearrange("p t (c i) -> p c t i", i=RUN),
                 in1=gain[:, g, :].unsqueeze(1).unsqueeze(3).to_broadcast([P, (hi - lo) // RUN, PACK, RUN]),
                 op=MULT,
             )
 
-        def scale_h_on_scalar(g, lo, hi, places=range(PACK)):
-            if (g, lo) not in h_rows:
-                h_rows[g, lo] = tile("h_rows%d_%d" % (g, lo), [P, PACK, hi - lo], BF16)
-            for t in places:
+        def scale_h_on_scalar(g, lo, hi):
+            h_rows[g, lo] = tile("h_rows%d_%d" % (g, lo), [P, PACK, hi - lo], BF16)
+            for t in range(PACK):
                 nc.scalar.activation(out=h_rows[g, lo][:, t, :], in_=sig_part(g, lo, hi)[:, t, :], func=COPY, scale=gain[:, g, t : t + 1])
 
-        def weave_h(engine, g, lo, hi, start=None):
-            start = lo if start is None else start
+        def weave_h(engine, g, lo, hi):
             copy(
                 engine,
-                h_bf[g][:, PACK * lo : PACK * hi].rearrange("p (c i t) -> p c t i", i=RUN, t=PACK),
-                h_rows[g, start][:, :, lo - start : hi - start].rearrange("p t (c i) -> p c t i", i=RUN),
-            )
-
-        def quant_h(g, lo, hi):
-            nc.vector.quantize_mx(
-                out=h_codes[g][:, lo:hi].bitcast(FP8X4), scales=h_scales[g][:, lo:hi], in_=h_bf[g][:, PACK * lo : PACK * hi]
+                rounded(("h", g), lo, hi).rearrange("p (c i t) -> p c t i", i=RUN, t=PACK),
+                h_rows[g, lo][:].rearrange("p t (c i) -> p c t i", i=RUN),
             )
 
         def second_product(g, lo, hi, bank):
-            s, c = divmod(g, 2)
             for col in range(lo, hi, NMM):
                 nc.tensor.matmul_mx(
                     out=y_banks[bank][:, col : col + NMM],
-                    lhsT=w2_codes[s][:, c * M : (c + 1) * M].bitcast(FP8X4),
-                    lhsT_scale=w2_scales[s][:, c * M : (c + 1) * M],
-                    rhs=h_codes[g][:, col : col + NMM].bitcast(FP8X4),
-                    rhs_scale=h_scales[g][:, col : col + NMM],
+                    lhsT=codes(("w2", g), 0, M),
+                    lhsT_scale=scales(("w2", g), 0, M),
+                    rhs=codes(("h", g), col, col + NMM),
+                    rhs_scale=scales(("h", g), col, col + NMM),
                     start=True,
                     stop=True,
                 )
@@ -245,124 +231,108 @@ def tile_rows_gmlp_sigmoid_bias_res_kernel(tc, x, w1, hs, w2, b, r, out):
 
         clear_vectors()
         warm_table()
-        load_w1(0, 0)
+        load_w1(0)
         load_vectors()
         load_x(0, 0)
         load_x(0, 1)
         load_x(0, 2)
-        load_w1(1, 0)
+        load_x(0, 3)
+        load_w1(1)
         load_x(1, 0)
         load_w2(0)
         load_w2(1)
         for g in range(G):
             load_r(g)
+
         round_w1("V", 0, 0)
         round_w1("S", 0, 1)
-        deal_vectors()
+        deal_vectors("V")
         round_x("V", 0, 0, 128)
+        quant(("w1", 0, 0), 0, 256)
+        quant(("x", 0), 0, 128)
+        quant(("w1", 0, 1), 0, 256)
         turn_vectors()
-        quant_w1(0, 0)
-        quant_x(0, 0, 128)
         round_x("S", 0, 128, 256)
         first_product(0, [0], 0, 128)
-        quant_w1(0, 1)
         first_product(0, [1], 0, 128)
-        first_product(1, [0, 1], 0, 128)
-        quant_w1(0, 2, 2)
         first_product(0, [2, 3], 0, 128)
+        first_product(1, [0, 1], 0, 128)
         first_product(1, [2, 3], 0, 128)
-        gather_gain()
-        quant_x(0, 128, 256)
-        for g in range(2):
-            sigmoid(g, 0, 0, 128)
-            sigmoid(g, 1, 0, 128)
+        round_x("V", 0, 256, 512, 0, 2)
+        quant(("x", 0), 128, 256)
+        gather_gain("V")
+        sigmoid(0, range(4), 0, 128)
         first_product(0, [0, 1], 128, 256)
         first_product(0, [2, 3], 128, 256)
+        sigmoid(1, range(4), 0, 128)
         first_product(1, [0, 1], 128, 256)
-        for g in range(2):
-            sigmoid(g, 2, 0, 128)
-            sigmoid(g, 3, 0, 128)
         first_product(1, [2, 3], 128, 256)
-        round_x("V", 0, 256, 384)
-        round_x("V", 0, 384, 512)
-        quant_x(0, 256, 384)
+        round_x("V", 0, 256, 512, 2, 4)
         scale_h(0, 0, 128)
-        quant_x(0, 384, 512)
-        first_product(0, [0, 1], 256, 512)
-        for t in range(4):
-            sigmoid(0, t, 128, 256)
+        quant(("x", 0), 256, 512)
+        first_product(0, [0], 256, 512)
+        sigmoid(0, range(4), 128, 256)
+        first_product(0, [1], 256, 512)
         first_product(0, [2, 3], 256, 512)
-        for t in range(4):
-            sigmoid(1, t, 128, 256)
+        sigmoid(1, range(4), 128, 256)
         first_product(1, [0, 1], 256, 512)
         first_product(1, [2, 3], 256, 512)
         scale_h(1, 0, 128)
-        round_w1("S", 1, 1, 0, 64)
         scale_h(0, 128, 256)
-        round_w1("V", 1, 1, 64, 128)
+
+        sigmoid(0, [0, 1], 256, 512)
         round_w1("V", 1, 0)
-        for t in range(4):
-            sigmoid(0, t, 256, 512)
-        sigmoid(1, 0, 256, 512)
-        sigmoid(1, 1, 256, 512)
-        scale_h_on_scalar(0, 384, 512)
-        round_x("S", 1, 384, 512)
-        sigmoid(1, 2, 256, 512)
-        sigmoid(1, 3, 256, 512)
-        weave_h("S", 0, 384, 512)
-        quant_w1(1, 2, 2)
-        quant_w1(1, 0, 2)
-        quant_h(0, 0, 256)
+        round_w1("S", 1, 1)
+        sigmoid(0, [2, 3], 256, 512)
+        scale_h(1, 128, 256)
+        quant(("w1", 1, 0), 0, 512)
+        quant(("w1", 1, 1), 0, 256)
+        round_x("S", 1, 256, 512)
         round_x("V", 1, 0, 256)
-        round_x("V", 1, 256, 384)
-        quant_x(1, 0, 256)
+        quant(("h", 1), 0, 256)
+        quant(("x", 1), 0, 256)
         first_product(2, [0, 1], 0, 256)
         first_product(2, [2, 3], 0, 256)
-        scale_h(1, 128, 256)
-        quant_x(1, 256, 512)
+        scale_h(0, 256, 512)
+        quant(("x", 1), 256, 512)
         first_product(2, [0, 1], 256, 512)
-        for t in range(4):
-            sigmoid(2, t, 0, 256)
+        sigmoid(1, range(4), 256, 512)
+        scale_h(1, 256, 512)
+        quant(("h", 0), 256, 512)
+        sigmoid(2, range(4), 0, 256)
         first_product(2, [2, 3], 256, 512)
         first_product(3, [0, 1], 0, 256)
         first_product(3, [2, 3], 0, 256)
         round_w2("S", 0)
-        scale_h(0, 256, 384)
-        scale_h(1, 256, 512)
-        quant_h(0, 256, 512)
         scale_h(2, 0, 256)
-        quant_w2(0)
+        quant(("w2", 0), 0, 128)
         second_product(0, 0, 512, 0)
-        quant_h(1, 0, 512)
-        for t in range(4):
-            sigmoid(2, t, 256, 512)
+        quant(("h", 1), 256, 512)
+        sigmoid(2, range(4), 256, 512)
         round_w2("S", 1)
         scale_h(2, 256, 512)
-        quant_w2(1)
+        quant(("w2", 1), 0, 128)
         finish(0, 0, 512, 0)
-        sigmoid(3, 0, 0, 256)
-        sigmoid(3, 1, 0, 256)
+        sigmoid(3, [0, 1], 0, 256)
         first_product(3, [0, 1], 256, 512)
-        sigmoid(3, 2, 0, 256)
-        sigmoid(3, 3, 0, 256)
+        sigmoid(3, [2, 3], 0, 256)
         first_product(3, [2, 3], 256, 512)
         second_product(1, 0, 512, 1)
         round_w2("S", 2)
-        quant_h(2, 0, 512)
+        quant(("h", 2), 0, 512)
         scale_h(3, 0, 256)
-        quant_w2(2)
+        quant(("w2", 2), 0, 128)
         second_product(2, 0, 512, 0)
         finish(1, 0, 512, 1)
-        for t in range(4):
-            sigmoid(3, t, 256, 512)
+        sigmoid(3, range(4), 256, 512)
         scale_h_on_scalar(3, 384, 512)
         round_w2("S", 3)
         weave_h("S", 3, 384, 512)
         scale_h(3, 256, 384)
-        quant_h(3, 0, 256)
-        quant_w2(3)
+        quant(("h", 3), 0, 256)
+        quant(("w2", 3), 0, 128)
         second_product(3, 0, 256, 1)
-        quant_h(3, 256, 512)
+        quant(("h", 3), 256, 512)
         second_product(3, 256, 512, 2)
         finish(2, 0, 256, 0)
         finish(2, 256, 512, 0)

@@ -23,7 +23,7 @@ RUN = 2
 NMM = 128
 WORDS = {"w1": 2 * P, "x": N, "w2": M, "h": N}
 Z_BANKS = (3, 2)
-X_PIECES = [[(0, 128, 0, 4), (128, 256, 0, 4), (256, 512, 0, 2), (256, 512, 2, 4)], [(0, 512, 0, 4)]]
+X_PIECES = [[(0, 128, 0, 4), (128, 256, 0, 4), (256, 512, 0, 4)], [(0, 512, 0, 4)]]
 STRIPS = [
     [("w1", 0, 0), ("w1", 0, 1)],
     [("x", 0)],
@@ -236,7 +236,6 @@ def tile_rows_gmlp_sigmoid_bias_res_kernel(tc, x, w1, hs, w2, b, r, out):
         load_x(0, 0)
         load_x(0, 1)
         load_x(0, 2)
-        load_x(0, 3)
         load_w1(1)
         load_x(1, 0)
         load_w2(0)
@@ -258,7 +257,6 @@ def tile_rows_gmlp_sigmoid_bias_res_kernel(tc, x, w1, hs, w2, b, r, out):
         first_product(0, [2, 3], 0, 128)
         first_product(1, [0, 1], 0, 128)
         first_product(1, [2, 3], 0, 128)
-        round_x("V", 0, 256, 512, 0, 2)
         quant(("x", 0), 128, 256)
         gather_gain("V")
         sigmoid(0, range(4), 0, 128)
@@ -267,7 +265,7 @@ def tile_rows_gmlp_sigmoid_bias_res_kernel(tc, x, w1, hs, w2, b, r, out):
         sigmoid(1, range(4), 0, 128)
         first_product(1, [0, 1], 128, 256)
         first_product(1, [2, 3], 128, 256)
-        round_x("V", 0, 256, 512, 2, 4)
+        round_x("V", 0, 256, 512)
         scale_h(0, 0, 128)
         quant(("x", 0), 256, 512)
         first_product(0, [0], 256, 512)

@@ -23,15 +23,16 @@ RUN = 2
 NMM = 128
 WORDS = {"w1": 2 * P, "x": N, "w2": M, "h": N}
 Z_BANKS = (3, 2)
-X_PIECES = [[(0, 128, 0, 4), (128, 256, 0, 4), (256, 512, 0, 4)], [(0, 512, 0, 4)]]
+X_PIECES = [[(0, 128, 0, 4), (128, 384, 0, 4), (384, 512, 0, 4)], [(0, 512, 0, 4)]]
 STRIPS = [
     [("w1", 0, 0), ("w1", 0, 1)],
     [("x", 0)],
     [("x", 1)],
     [("w1", 1, 1), ("w1", 1, 0), ("h", 0)],
-    [("h", 1), ("w2", 0)],
-    [("w2", 1), ("h", 2), ("w2", 2)],
-    [("w2", 3), ("h", 3)],
+    [("h", 1)],
+    [("h", 2)],
+    [("h", 3)],
+    [("w2", 0), ("w2", 1), ("w2", 2), ("w2", 3)],
 ]
 
 
@@ -251,26 +252,28 @@ def tile_rows_gmlp_sigmoid_bias_res_kernel(tc, x, w1, hs, w2, b, r, out):
         quant(("x", 0), 0, 128)
         quant(("w1", 0, 1), 0, 256)
         turn_vectors()
-        round_x("S", 0, 128, 256)
         first_product(0, [0], 0, 128)
         first_product(0, [1], 0, 128)
         first_product(0, [2, 3], 0, 128)
         first_product(1, [0, 1], 0, 128)
         first_product(1, [2, 3], 0, 128)
-        quant(("x", 0), 128, 256)
+        round_x("S", 0, 128, 192)
+        round_x("V", 0, 192, 256)
+        round_x("V", 0, 256, 384)
         gather_gain("V")
+        quant(("x", 0), 128, 256)
         sigmoid(0, range(4), 0, 128)
         first_product(0, [0, 1], 128, 256)
         first_product(0, [2, 3], 128, 256)
         sigmoid(1, range(4), 0, 128)
         first_product(1, [0, 1], 128, 256)
         first_product(1, [2, 3], 128, 256)
-        round_x("V", 0, 256, 512)
+        round_x("V", 0, 384, 512)
+        quant(("x", 0), 256, 384)
         scale_h(0, 0, 128)
-        quant(("x", 0), 256, 512)
-        first_product(0, [0], 256, 512)
+        quant(("x", 0), 384, 512)
+        first_product(0, [0, 1], 256, 512)
         sigmoid(0, range(4), 128, 256)
-        first_product(0, [1], 256, 512)
         first_product(0, [2, 3], 256, 512)
         sigmoid(1, range(4), 128, 256)
         first_product(1, [0, 1], 256, 512)
@@ -278,15 +281,14 @@ def tile_rows_gmlp_sigmoid_bias_res_kernel(tc, x, w1, hs, w2, b, r, out):
         scale_h(1, 0, 128)
         scale_h(0, 128, 256)
 
-        sigmoid(0, [0, 1], 256, 512)
         round_w1("V", 1, 0)
         round_w1("S", 1, 1)
-        sigmoid(0, [2, 3], 256, 512)
+        sigmoid(0, range(4), 256, 512)
         scale_h(1, 128, 256)
         quant(("w1", 1, 0), 0, 512)
         quant(("w1", 1, 1), 0, 256)
-        round_x("S", 1, 256, 512)
-        round_x("V", 1, 0, 256)
+        round_x("S", 1, 288, 512)
+        round_x("V", 1, 0, 288)
         quant(("h", 1), 0, 256)
         quant(("x", 1), 0, 256)
         first_product(2, [0, 1], 0, 256)
@@ -295,38 +297,37 @@ def tile_rows_gmlp_sigmoid_bias_res_kernel(tc, x, w1, hs, w2, b, r, out):
         quant(("x", 1), 256, 512)
         first_product(2, [0, 1], 256, 512)
         sigmoid(1, range(4), 256, 512)
+        round_w2("S", 0)
         scale_h(1, 256, 512)
         quant(("h", 0), 256, 512)
+        quant(("w2", 0), 0, 128)
         sigmoid(2, range(4), 0, 256)
         first_product(2, [2, 3], 256, 512)
         first_product(3, [0, 1], 0, 256)
         first_product(3, [2, 3], 0, 256)
-        round_w2("S", 0)
-        scale_h(2, 0, 256)
-        quant(("w2", 0), 0, 128)
         second_product(0, 0, 512, 0)
+        scale_h(2, 0, 256)
         quant(("h", 1), 256, 512)
         sigmoid(2, range(4), 256, 512)
-        round_w2("S", 1)
         scale_h(2, 256, 512)
-        quant(("w2", 1), 0, 128)
         finish(0, 0, 512, 0)
         sigmoid(3, [0, 1], 0, 256)
         first_product(3, [0, 1], 256, 512)
         sigmoid(3, [2, 3], 0, 256)
         first_product(3, [2, 3], 256, 512)
-        second_product(1, 0, 512, 1)
+        round_w2("S", 1)
         round_w2("S", 2)
         quant(("h", 2), 0, 512)
-        scale_h(3, 0, 256)
-        quant(("w2", 2), 0, 128)
+        quant(("w2", 1), 0, 256)
+        second_product(1, 0, 512, 1)
         second_product(2, 0, 512, 0)
-        finish(1, 0, 512, 1)
+        scale_h(3, 0, 256)
         sigmoid(3, range(4), 256, 512)
-        scale_h_on_scalar(3, 384, 512)
+        scale_h_on_scalar(3, 368, 512)
         round_w2("S", 3)
-        weave_h("S", 3, 384, 512)
-        scale_h(3, 256, 384)
+        weave_h("S", 3, 368, 512)
+        scale_h(3, 256, 368)
+        finish(1, 0, 512, 1)
         quant(("h", 3), 0, 256)
         quant(("w2", 3), 0, 128)
         second_product(3, 0, 256, 1)

@@ -75,7 +75,7 @@ def tile_rows_gmlp_sigmoid_bias_res_kernel(tc, x, w1, hs, w2, b, r, out):
             (s, lo, j0): tile("x_raw%d_%d_%d" % (s, lo, j0), [P, j1 - j0, hi - lo], F32) for s in range(PAIRS) for lo, hi, j0, j1 in X_PIECES[s]
         }
         w2_raw = [tile("w2_raw%d" % s, [P, 2, PACK, M], F32) for s in range(PAIRS)]
-        r_sb = [tile("r_sb%d" % g, [P, N], F32) for g in range(G)]
+        r_sb = tile("r_sb", [P, G * N], F32)
         vec_rows = tile("vec_rows", [P, P], F32)
         vec_dealt = tile("vec_dealt", [P, P], F32)
         vec_turned = tile("vec_turned", [P, P], F32)
@@ -107,8 +107,8 @@ def tile_rows_gmlp_sigmoid_bias_res_kernel(tc, x, w1, hs, w2, b, r, out):
                 in_=w2[2 * s : 2 * s + 2].rearrange("g (p j) m -> p g (j m)", j=PACK),
             )
 
-        def load_r(g):
-            nc.sync.dma_start(out=r_sb[g][:], in_=r[g])
+        def load_r():
+            nc.sync.dma_start(out=r_sb[:].rearrange("p (g n) -> p g n", g=G), in_=r.rearrange("g m n -> m g n"))
 
         def load_vectors():
             for v, src in enumerate((b, hs)):
@@ -227,7 +227,7 @@ def tile_rows_gmlp_sigmoid_bias_res_kernel(tc, x, w1, hs, w2, b, r, out):
                 )
 
         def finish(g, lo, hi, bank):
-            nc.vector.tensor_tensor(out=y_sb[g][:, lo:hi], in0=y_banks[bank][:, lo:hi], in1=r_sb[g][:, lo:hi], op=ADD)
+            nc.vector.tensor_tensor(out=y_sb[g][:, lo:hi], in0=y_banks[bank][:, lo:hi], in1=r_sb[:, g * N + lo : g * N + hi], op=ADD)
             nc.sync.dma_start(out=out[g][:, lo:hi], in_=y_sb[g][:, lo:hi])
 
         clear_vectors()
@@ -241,8 +241,7 @@ def tile_rows_gmlp_sigmoid_bias_res_kernel(tc, x, w1, hs, w2, b, r, out):
         load_x(1, 0)
         load_w2(0)
         load_w2(1)
-        for g in range(G):
-            load_r(g)
+        load_r()
 
         round_w1("V", 0, 0)
         round_w1("S", 0, 1)
@@ -257,10 +256,9 @@ def tile_rows_gmlp_sigmoid_bias_res_kernel(tc, x, w1, hs, w2, b, r, out):
         first_product(0, [2, 3], 0, 128)
         first_product(1, [0, 1], 0, 128)
         first_product(1, [2, 3], 0, 128)
-        round_x("S", 0, 128, 192)
-        round_x("V", 0, 192, 256)
+        gather_gain("S")
+        round_x("V", 0, 128, 256)
         round_x("V", 0, 256, 384)
-        gather_gain("V")
         quant(("x", 0), 128, 256)
         sigmoid(0, range(4), 0, 128)
         first_product(0, [0, 1], 128, 256)
@@ -272,12 +270,12 @@ def tile_rows_gmlp_sigmoid_bias_res_kernel(tc, x, w1, hs, w2, b, r, out):
         quant(("x", 0), 256, 384)
         scale_h(0, 0, 128)
         quant(("x", 0), 384, 512)
-        first_product(0, [0, 1], 256, 512)
-        sigmoid(0, range(4), 128, 256)
         first_product(0, [2, 3], 256, 512)
+        sigmoid(0, range(4), 128, 256)
+        first_product(0, [0, 1], 256, 512)
         sigmoid(1, range(4), 128, 256)
-        first_product(1, [0, 1], 256, 512)
         first_product(1, [2, 3], 256, 512)
+        first_product(1, [0, 1], 256, 512)
         scale_h(1, 0, 128)
         scale_h(0, 128, 256)
 

@@ -75,7 +75,7 @@ def tile_rows_gmlp_sigmoid_bias_res_kernel(tc, x, w1, hs, w2, b, r, out):
             (s, lo, j0): tile("x_raw%d_%d_%d" % (s, lo, j0), [P, j1 - j0, hi - lo], F32) for s in range(PAIRS) for lo, hi, j0, j1 in X_PIECES[s]
         }
         w2_raw = [tile("w2_raw%d" % s, [P, 2, PACK, M], F32) for s in range(PAIRS)]
-        r_sb = tile("r_sb", [P, G * N], F32)
+        r_sb = [tile("r_sb%d" % g, [P, N], F32) for g in range(G)]
         vec_rows = tile("vec_rows", [P, P], F32)
         vec_dealt = tile("vec_dealt", [P, P], F32)
         vec_turned = tile("vec_turned", [P, P], F32)
@@ -107,8 +107,8 @@ def tile_rows_gmlp_sigmoid_bias_res_kernel(tc, x, w1, hs, w2, b, r, out):
                 in_=w2[2 * s : 2 * s + 2].rearrange("g (p j) m -> p g (j m)", j=PACK),
             )
 
-        def load_r():
-            nc.sync.dma_start(out=r_sb[:].rearrange("p (g n) -> p g n", g=G), in_=r.rearrange("g m n -> m g n"))
+        def load_r(g):
+            nc.sync.dma_start(out=r_sb[g][:], in_=r[g])
 
         def load_vectors():
             for v, src in enumerate((b, hs)):
@@ -227,7 +227,7 @@ def tile_rows_gmlp_sigmoid_bias_res_kernel(tc, x, w1, hs, w2, b, r, out):
                 )
 
         def finish(g, lo, hi, bank):
-            nc.vector.tensor_tensor(out=y_sb[g][:, lo:hi], in0=y_banks[bank][:, lo:hi], in1=r_sb[:, g * N + lo : g * N + hi], op=ADD)
+            nc.vector.tensor_tensor(out=y_sb[g][:, lo:hi], in0=y_banks[bank][:, lo:hi], in1=r_sb[g][:, lo:hi], op=ADD)
             nc.sync.dma_start(out=out[g][:, lo:hi], in_=y_sb[g][:, lo:hi])
 
         clear_vectors()
@@ -241,7 +241,8 @@ def tile_rows_gmlp_sigmoid_bias_res_kernel(tc, x, w1, hs, w2, b, r, out):
         load_x(1, 0)
         load_w2(0)
         load_w2(1)
-        load_r()
+        for g in range(G):
+            load_r(g)
 
         round_w1("V", 0, 0)
         round_w1("S", 0, 1)

@@ -21,6 +21,7 @@ ROWS = 64
 PAIRS = 2
 RUN = 2
 NMM = 128
+STORE = 256
 WORDS = {"w1": 2 * P, "x": N, "w2": M, "h": N}
 Z_BANKS = (3, 2)
 X_PIECES = [[(0, 128, 0, 4), (128, 384, 0, 4), (384, 512, 0, 4)], [(0, 512, 0, 4)]]
@@ -74,7 +75,7 @@ def tile_rows_gmlp_sigmoid_bias_res_kernel(tc, x, w1, hs, w2, b, r, out):
         x_raw = {
             (s, lo, j0): tile("x_raw%d_%d_%d" % (s, lo, j0), [P, j1 - j0, hi - lo], F32) for s in range(PAIRS) for lo, hi, j0, j1 in X_PIECES[s]
         }
-        w2_raw = [tile("w2_raw%d" % s, [P, 2, PACK, M], F32) for s in range(PAIRS)]
+        w2_raw = [tile("w2_raw%d" % g, [P, PACK, M], F32) for g in range(G)]
         r_sb = [tile("r_sb%d" % g, [P, N], F32) for g in range(G)]
         vec_rows = tile("vec_rows", [P, P], F32)
         vec_dealt = tile("vec_dealt", [P, P], F32)
@@ -101,11 +102,8 @@ def tile_rows_gmlp_sigmoid_bias_res_kernel(tc, x, w1, hs, w2, b, r, out):
             lo, hi, j0, j1 = X_PIECES[s][i]
             nc.sync.dma_start(out=x_raw[s, lo, j0][:], in_=pair(x, s)[:, j0:j1, lo:hi])
 
-        def load_w2(s):
-            nc.sync.dma_start(
-                out=w2_raw[s][:].rearrange("p g j m -> p g (j m)"),
-                in_=w2[2 * s : 2 * s + 2].rearrange("g (p j) m -> p g (j m)", j=PACK),
-            )
+        def load_w2(g):
+            nc.sync.dma_start(out=w2_raw[g][:], in_=w2[g].rearrange("(p j) m -> p j m", j=PACK))
 
         def load_r(g):
             nc.sync.dma_start(out=r_sb[g][:], in_=r[g])
@@ -152,11 +150,10 @@ def tile_rows_gmlp_sigmoid_bias_res_kernel(tc, x, w1, hs, w2, b, r, out):
             )
 
         def round_w2(engine, g):
-            s, c = divmod(g, 2)
             copy(
                 engine,
                 rounded(("w2", g), 0, M).rearrange("p (c i j) -> p c j i", i=RUN, j=PACK),
-                w2_raw[s][:, c].rearrange("p j (c i) -> p c j i", i=RUN),
+                w2_raw[g][:].rearrange("p j (c i) -> p c j i", i=RUN),
             )
 
         def first_product(g, places, lo, hi):
@@ -228,7 +225,8 @@ def tile_rows_gmlp_sigmoid_bias_res_kernel(tc, x, w1, hs, w2, b, r, out):
 
         def finish(g, lo, hi, bank):
             nc.vector.tensor_tensor(out=y_sb[g][:, lo:hi], in0=y_banks[bank][:, lo:hi], in1=r_sb[g][:, lo:hi], op=ADD)
-            nc.sync.dma_start(out=out[g][:, lo:hi], in_=y_sb[g][:, lo:hi])
+            for col in range(lo, hi, STORE):
+                nc.sync.dma_start(out=out[g][:, col : col + STORE], in_=y_sb[g][:, col : col + STORE])
 
         clear_vectors()
         warm_table()
@@ -241,8 +239,12 @@ def tile_rows_gmlp_sigmoid_bias_res_kernel(tc, x, w1, hs, w2, b, r, out):
         load_x(1, 0)
         load_w2(0)
         load_w2(1)
-        for g in range(G):
-            load_r(g)
+        load_w2(2)
+        load_r(0)
+        load_w2(3)
+        load_r(1)
+        load_r(2)
+        load_r(3)
 
         round_w1("V", 0, 0)
         round_w1("S", 0, 1)

@@ -231,8 +231,8 @@ def tile_rows_gmlp_sigmoid_bias_res_kernel(tc, x, w1, hs, w2, b, r, out):
         clear_vectors()
         warm_table()
         load_w1(0)
-        load_vectors()
         load_x(0, 0)
+        load_vectors()
         load_x(0, 1)
         load_x(0, 2)
         load_w1(1)
@@ -248,8 +248,8 @@ def tile_rows_gmlp_sigmoid_bias_res_kernel(tc, x, w1, hs, w2, b, r, out):
 
         round_w1("V", 0, 0)
         round_w1("S", 0, 1)
-        deal_vectors("V")
         round_x("V", 0, 0, 128)
+        deal_vectors("S")
         quant(("w1", 0, 0), 0, 256)
         quant(("x", 0), 0, 128)
         quant(("w1", 0, 1), 0, 256)
@@ -288,8 +288,8 @@ def tile_rows_gmlp_sigmoid_bias_res_kernel(tc, x, w1, hs, w2, b, r, out):
         scale_h(1, 128, 256)
         quant(("w1", 1, 0), 0, 512)
         quant(("w1", 1, 1), 0, 256)
-        round_x("S", 1, 288, 512)
-        round_x("V", 1, 0, 288)
+        round_x("S", 1, 304, 512)
+        round_x("V", 1, 0, 304)
         quant(("h", 1), 0, 256)
         quant(("x", 1), 0, 256)
         first_product(2, [0, 1], 0, 256)
@@ -324,10 +324,10 @@ def tile_rows_gmlp_sigmoid_bias_res_kernel(tc, x, w1, hs, w2, b, r, out):
         second_product(2, 0, 512, 0)
         scale_h(3, 0, 256)
         sigmoid(3, range(4), 256, 512)
-        scale_h_on_scalar(3, 368, 512)
+        scale_h_on_scalar(3, 384, 512)
         round_w2("S", 3)
-        weave_h("S", 3, 368, 512)
-        scale_h(3, 256, 368)
+        weave_h("S", 3, 384, 512)
+        scale_h(3, 256, 384)
         finish(1, 0, 512, 1)
         quant(("h", 3), 0, 256)
         quant(("w2", 3), 0, 128)

from contextlib import ExitStack

import concourse.mybir as mybir

G, D, K, M, N = 4, 256, 512, 128, 512
FLOPS = 2 * G * N * K * (D + M)

F32 = mybir.dt.float32
BF16 = mybir.dt.bfloat16
U32 = mybir.dt.uint32
U8 = mybir.dt.uint8
FP8X4 = mybir.dt.float8_e4m3fn_x4
SIGMOID = mybir.ActivationFunctionType.Sigmoid
COPY = mybir.ActivationFunctionType.Copy
MULT = mybir.AluOpType.mult
ADD = mybir.AluOpType.add

P = 128
PACK = 4
ROWS = 64
PAIRS = 2
RUN = 2
NMM = 128
STORE = 256
WORDS = {"w1": 2 * P, "x": N, "w2": M, "h": N}
Z_BANKS = (3, 2)
X_PIECES = [[(0, 128, 0, 4), (128, 384, 0, 4), (384, 512, 0, 4)], [(0, 512, 0, 4)]]
STRIPS = [
    [("w1", 0, 0), ("w1", 0, 1)],
    [("x", 0)],
    [("x", 1)],
    [("w1", 1, 1), ("w1", 1, 0), ("h", 0)],
    [("h", 1)],
    [("h", 2)],
    [("h", 3)],
    [("w2", 0), ("w2", 1), ("w2", 2), ("w2", 3)],
]


def tile_rows_gmlp_sigmoid_bias_res_kernel(tc, x, w1, hs, w2, b, r, out):
    nc = tc.nc
    with ExitStack() as ctx:
        sb = ctx.enter_context(tc.tile_pool(name="sb", bufs=1))
        ps = ctx.enter_context(tc.psum_pool(name="ps", bufs=1))
        ctx.enter_context(tc.manual_schedule())

        def tile(name, shape, dtype):
            return sb.tile(shape, dtype, name=name, align_bytes=64)

        place = {}
        for i, names in enumerate(STRIPS):
            words = sum(WORDS[name[0]] for name in names)
            strip = (tile("rounded%d" % i, [P, PACK * words], BF16), tile("codes%d" % i, [P, words], U32), tile("scales%d" % i, [P, words], U8))
            start = 0
            for name in names:
                place[name] = (strip, start)
                start = start + WORDS[name[0]]

        def rounded(name, lo, hi):
            strip, start = place[name]
            return strip[0][:, PACK * (start + lo) : PACK * (start + hi)]

        def codes(name, lo, hi, rows=slice(0, P)):
            strip, start = place[name]
            return strip[1][rows, start + lo : start + hi].bitcast(FP8X4)

        def scales(name, lo, hi, rows=slice(0, P)):
            strip, start = place[name]
            return strip[2][rows, start + lo : start + hi]

        def quant(name, lo, hi):
            nc.vector.quantize_mx(out=codes(name, lo, hi), scales=scales(name, lo, hi), in_=rounded(name, lo, hi))

        w1_raw = [tile("w1_raw%d" % s, [P, PACK, K], F32) for s in range(PAIRS)]
        x_raw = {
            (s, lo, j0): tile("x_raw%d_%d_%d" % (s, lo, j0), [P, j1 - j0, hi - lo], F32) for s in range(PAIRS) for lo, hi, j0, j1 in X_PIECES[s]
        }
        w2_raw = [tile("w2_raw%d" % g, [P, PACK, M], F32) for g in range(G)]
        r_sb = [tile("r_sb%d" % g, [P, N], F32) for g in range(G)]
        vec_rows = tile("vec_rows", [P, P], F32)
        vec_dealt = tile("vec_dealt", [P, P], F32)
        vec_turned = tile("vec_turned", [P, P], F32)
        warm = tile("warm", [P, 2], F32)
        gain = tile("gain", [P, G, PACK], F32)

        sig = {}
        h_rows = {}
        y_sb = [tile("y_sb%d" % g, [P, N], F32) for g in range(G)]

        z_banks = [[ps.tile([P, N], F32, name="z%d%d" % (c, i)) for i in range(Z_BANKS[c])] for c in range(2)]
        y_banks = [ps.tile([P, N], F32, name="y%d" % i) for i in range(8 - sum(Z_BANKS))]
        z_turn = [0, 0]
        z_place = {}

        def pair(t, s):
            return t[2 * s : 2 * s + 2].rearrange("g (p j) n -> (g p) j n", j=PACK)

        def load_w1(s):
            nc.sync.dma_start(out=w1_raw[s][:], in_=pair(w1, s))

        def load_x(s, i):
            lo, hi, j0, j1 = X_PIECES[s][i]
            nc.sync.dma_start(out=x_raw[s, lo, j0][:], in_=pair(x, s)[:, j0:j1, lo:hi])

        def load_w2(g):
            nc.sync.dma_start(out=w2_raw[g][:], in_=w2[g].rearrange("(p j) m -> p j m", j=PACK))

        def load_r(g):
            nc.sync.dma_start(out=r_sb[g][:], in_=r[g])

        def load_vectors():
            for v, src in enumerate((b, hs)):
                nc.sync.dma_start(out=vec_rows[4 * v : P : 8, :], in_=src.rearrange("g (q a) o -> q g (a o)", q=4))

        def warm_table():
            nc.vector.memset(warm[:, 0:1], 0.0)
            nc.scalar.activation(out=warm[:, 1:2], in_=warm[:, 0:1], func=SIGMOID)

        def clear_vectors():
            nc.vector.memset(vec_rows[:], 0.0)

        def copy(engine, dst, src):
            if engine == "V":
                nc.vector.tensor_copy(out=dst, in_=src)
            else:
                nc.scalar.copy(out=dst, in_=src)

        def deal_vectors(engine):
            copy(engine, vec_dealt[:].rearrange("p (t s) -> p t s", t=PACK), vec_rows[:].rearrange("p (s t) -> p t s", t=PACK))

        def turn_vectors():
            nc.vector.transpose(out=vec_turned[:], in_=vec_dealt[:])

        def gather_gain(engine):
            copy(engine, gain[:], vec_turned[:].rearrange("p (t g z) -> p g t z", t=PACK, g=G)[:, :, :, 4])

        def round_w1(engine, s, u, a=0, z=P):
            copy(
                engine,
                rounded(("w1", s, u), 0, 2 * P).rearrange("p (e m j) -> p m j e", e=2, j=PACK)[:, a:z],
                w1_raw[s][:].rearrange("p j (m u e) -> p u m j e", u=2, e=2)[:, u, a:z],
            )

        def round_x(engine, s, lo, hi, j0=0, j1=PACK):
            start = max(piece[0] for piece in X_PIECES[s] if piece[0] <= lo)
            copy(
                engine,
                rounded(("x", s), lo, hi).rearrange("p (c i j) -> p c j i", i=RUN, j=PACK)[:, :, j0:j1],
                x_raw[s, start, j0][:, :, lo - start : hi - start].rearrange("p j (c i) -> p c j i", i=RUN),
            )

        def round_w2(engine, g):
            copy(
                engine,
                rounded(("w2", g), 0, M).rearrange("p (c i j) -> p c j i", i=RUN, j=PACK),
                w2_raw[g][:].rearrange("p j (c i) -> p c j i", i=RUN),
            )

        def first_product(g, places, lo, hi):
            s, c = divmod(g, 2)
            rows = slice(c * ROWS, (c + 1) * ROWS)
            bank = z_banks[c][z_turn[c] % Z_BANKS[c]]
            z_turn[c] = z_turn[c] + 1
            for n, t in enumerate(places):
                base = n * (hi - lo) - lo
                z_place[g, t, lo] = (bank, base)
                for col in range(lo, hi, NMM):
                    nc.tensor.matmul_mx(
                        out=bank[:, base + col : base + col + NMM],
                        lhsT=codes(("w1", s, t // 2), t % 2 * P, (t % 2 + 1) * P, rows),
                        lhsT_scale=scales(("w1", s, t // 2), t % 2 * P, (t % 2 + 1) * P, rows),
                        rhs=codes(("x", s), col, col + NMM, rows),
                        rhs_scale=scales(("x", s), col, col + NMM, rows),
                        start=True,
                        stop=True,
                    )

        def sigmoid(g, places, lo, hi):
            if (g, lo) not in sig:
                sig[g, lo] = tile("sig%d_%d" % (g, lo), [P, PACK, hi - lo], F32)
            for t in places:
                bank, base = z_place[g, t, lo]
                nc.scalar.activation(
                    out=sig[g, lo][:, t, :],
                    in_=bank[:, base + lo : base + hi],
                    func=SIGMOID,
                    bias=vec_turned[:, 32 * t + 8 * g : 32 * t + 8 * g + 1],
                )

        def sig_part(g, lo, hi):
            start = max(a for q, a in sig if q == g and a <= lo)
            return sig[g, start][:, :, lo - start : hi - start]

        def scale_h(g, lo, hi):
            nc.vector.tensor_tensor(
                out=rounded(("h", g), lo, hi).rearrange("p (c i t) -> p c t i", i=RUN, t=PACK),
                in0=sig_part(g, lo, hi).rearrange("p t (c i) -> p c t i", i=RUN),
                in1=gain[:, g, :].unsqueeze(1).unsqueeze(3).to_broadcast([P, (hi - lo) // RUN, PACK, RUN]),
                op=MULT,
            )

        def scale_h_on_scalar(g, lo, hi):
            h_rows[g, lo] = tile("h_rows%d_%d" % (g, lo), [P, PACK, hi - lo], BF16)
            for t in range(PACK):
                nc.scalar.activation(out=h_rows[g, lo][:, t, :], in_=sig_part(g, lo, hi)[:, t, :], func=COPY, scale=gain[:, g, t : t + 1])

        def weave_h(engine, g, lo, hi):
            copy(
                engine,
                rounded(("h", g), lo, hi).rearrange("p (c i t) -> p c t i", i=RUN, t=PACK),
                h_rows[g, lo][:].rearrange("p t (c i) -> p c t i", i=RUN),
            )

        def second_product(g, lo, hi, bank):
            for col in range(lo, hi, NMM):
                nc.tensor.matmul_mx(
                    out=y_banks[bank][:, col : col + NMM],
                    lhsT=codes(("w2", g), 0, M),
                    lhsT_scale=scales(("w2", g), 0, M),
                    rhs=codes(("h", g), col, col + NMM),
                    rhs_scale=scales(("h", g), col, col + NMM),
                    start=True,
                    stop=True,
                )

        def finish(g, lo, hi, bank):
            nc.vector.tensor_tensor(out=y_sb[g][:, lo:hi], in0=y_banks[bank][:, lo:hi], in1=r_sb[g][:, lo:hi], op=ADD)
            for col in range(lo, hi, STORE):
                nc.sync.dma_start(out=out[g][:, col : col + STORE], in_=y_sb[g][:, col : col + STORE])

        clear_vectors()
        warm_table()
        load_w1(0)
        load_x(0, 0)
        load_vectors()
        load_x(0, 1)
        load_x(0, 2)
        load_w1(1)
        load_x(1, 0)
        load_w2(0)
        load_w2(1)
        load_w2(2)
        load_r(0)
        load_w2(3)
        load_r(1)
        load_r(2)
        load_r(3)

        round_w1("V", 0, 0)
        round_w1("S", 0, 1)
        round_x("V", 0, 0, 128)
        deal_vectors("S")
        quant(("w1", 0, 0), 0, 256)
        quant(("x", 0), 0, 128)
        quant(("w1", 0, 1), 0, 256)
        turn_vectors()
        first_product(0, [0], 0, 128)
        first_product(0, [1], 0, 128)
        first_product(0, [2, 3], 0, 128)
        first_product(1, [0, 1], 0, 128)
        first_product(1, [2, 3], 0, 128)
        gather_gain("S")
        round_x("V", 0, 128, 256)
        round_x("V", 0, 256, 384)
        quant(("x", 0), 128, 256)
        sigmoid(0, range(4), 0, 128)
        first_product(0, [0, 1], 128, 256)
        first_product(0, [2, 3], 128, 256)
        sigmoid(1, range(4), 0, 128)
        first_product(1, [0, 1], 128, 256)
        first_product(1, [2, 3], 128, 256)
        round_x("V", 0, 384, 512)
        quant(("x", 0), 256, 384)
        scale_h(0, 0, 128)
        quant(("x", 0), 384, 512)
        first_product(0, [2, 3], 256, 512)
        sigmoid(0, range(4), 128, 256)
        first_product(0, [0, 1], 256, 512)
        sigmoid(1, range(4), 128, 256)
        first_product(1, [2, 3], 256, 512)
        first_product(1, [0, 1], 256, 512)
        scale_h(1, 0, 128)
        scale_h(0, 128, 256)

        round_w1("V", 1, 0)
        round_w1("S", 1, 1)
        sigmoid(0, range(4), 256, 512)
        scale_h(1, 128, 256)
        quant(("w1", 1, 0), 0, 512)
        quant(("w1", 1, 1), 0, 256)
        round_x("S", 1, 304, 512)
        round_x("V", 1, 0, 304)
        quant(("h", 1), 0, 256)
        quant(("x", 1), 0, 256)
        first_product(2, [0, 1], 0, 256)
        first_product(2, [2, 3], 0, 256)
        scale_h(0, 256, 512)
        quant(("x", 1), 256, 512)
        first_product(2, [0, 1], 256, 512)
        sigmoid(1, range(4), 256, 512)
        round_w2("S", 0)
        scale_h(1, 256, 512)
        quant(("h", 0), 256, 512)
        quant(("w2", 0), 0, 128)
        sigmoid(2, range(4), 0, 256)
        first_product(2, [2, 3], 256, 512)
        first_product(3, [0, 1], 0, 256)
        first_product(3, [2, 3], 0, 256)
        second_product(0, 0, 512, 0)
        scale_h(2, 0, 256)
        quant(("h", 1), 256, 512)
        sigmoid(2, range(4), 256, 512)
        scale_h(2, 256, 512)
        finish(0, 0, 512, 0)
        sigmoid(3, [0, 1], 0, 256)
        first_product(3, [0, 1], 256, 512)
        sigmoid(3, [2, 3], 0, 256)
        first_product(3, [2, 3], 256, 512)
        round_w2("S", 1)
        round_w2("S", 2)
        quant(("h", 2), 0, 512)
        quant(("w2", 1), 0, 256)
        second_product(1, 0, 512, 1)
        second_product(2, 0, 512, 0)
        scale_h(3, 0, 256)
        sigmoid(3, range(4), 256, 512)
        scale_h_on_scalar(3, 384, 512)
        round_w2("S", 3)
        weave_h("S", 3, 384, 512)
        scale_h(3, 256, 384)
        finish(1, 0, 512, 1)
        quant(("h", 3), 0, 256)
        quant(("w2", 3), 0, 128)
        second_product(3, 0, 256, 1)
        quant(("h", 3), 256, 512)
        second_product(3, 256, 512, 2)
        finish(2, 0, 256, 0)
        finish(2, 256, 512, 0)
        finish(3, 0, 256, 1)
        finish(3, 256, 512, 2)
